import numpy as np
import ml_dtypes


def mxq(x, axis, fmt="e4m3"):
    dtype, down = {"e4m3": (ml_dtypes.float8_e4m3fn, 7), "e5m2": (ml_dtypes.float8_e5m2, 14)}[fmt]
    v = np.moveaxis(np.asarray(x, np.float32).astype(ml_dtypes.bfloat16).astype(np.float64), axis, -1)
    blocks = v.reshape(v.shape[:-1] + (-1, 32))
    amax = np.abs(blocks).max(-1, keepdims=True)
    byte = np.maximum(np.where(amax > 0, np.frexp(amax)[1] - 1 + 127, 0) - down, 1)
    scale = np.exp2(byte - 127.0)
    codes = (blocks / scale).astype(np.float32).astype(dtype).astype(np.float64)
    return np.moveaxis((codes * scale).reshape(v.shape), -1, axis)


WIDE = False


def mx_kscale(k):
    if not WIDE:
        return np.ones(k)
    levels = np.array([10, -10, 5, -5, 0])
    if k % 512:
        return np.exp2(np.random.permutation(np.resize(levels, k // 32))).repeat(32)
    a = np.empty((k // 512, 16))
    for p in range(k // 512):
        a[p, :8] = np.random.permutation(np.resize(levels, 8))
        for g in range(8):
            far = levels[np.abs(levels - a[p, g]) >= 10]
            a[p, g + 8] = far[np.random.randint(len(far))]
    return np.exp2(a.ravel()).repeat(32)


def f64(x):
    return np.asarray(x).astype(np.float64)


def striped(idx):
    return np.tile(idx.reshape(-1, 16).T, (8, 1)).astype(np.uint16)


def unstriped(offs):
    return offs[:16].T.reshape(-1).astype(np.int64)


E2M1 = np.array([0.0, 0.5, 1.0, 1.5, 2.0, 3.0, 4.0, 6.0, -0.0, -0.5, -1.0, -1.5, -2.0, -3.0, -4.0, -6.0])


def pack_weight(w, fmt):
    k, n = w.shape
    w = f64(np.asarray(w, np.float32).astype(ml_dtypes.bfloat16)).reshape(k // 32, 32, n)
    amax = np.abs(w).max(1)
    if fmt == "e4m3":
        byte = np.frexp(amax)[1] - 1 + 127 - 7
    else:
        mant, ex = np.frexp(amax / 6.0)
        byte = np.where(mant > 0.5, ex, ex - 1) + 127
    byte = np.clip(np.where(amax > 0, byte, 1), 1, 254)
    scaled = (w * np.exp2(127.0 - byte)[:, None, :]).reshape(k, n).astype(np.float32)
    by_word = np.ascontiguousarray(scaled.reshape(k // 512, 128, 4, n).transpose(0, 1, 3, 2))
    if fmt == "e4m3":
        words = by_word.astype(ml_dtypes.float8_e4m3fn).view(np.uint8)
    else:
        c = by_word.astype(ml_dtypes.float4_e2m1fn).view(np.uint8) & 0xF
        words = (c[..., 0::2] | (c[..., 1::2] << 4)).reshape(k // 512, 128, 2 * n)
    return np.ascontiguousarray(words), np.ascontiguousarray(byte.astype(np.uint8).reshape(k // 512, 16, n))


def unpack_weight(words, scales, fmt):
    g, _, n = scales.shape
    words = np.ascontiguousarray(words).reshape(g, 128, n, -1)
    if fmt == "e4m3":
        vals = words.view(ml_dtypes.float8_e4m3fn).astype(np.float64)
    else:
        nib = np.empty((g, 128, n, 4), np.uint8)
        nib[..., 0::2] = words & 0xF
        nib[..., 1::2] = words >> 4
        vals = E2M1[nib]
    vals = vals * np.repeat(np.exp2(scales.astype(np.float64) - 127.0), 8, axis=1)[..., None]
    return vals.transpose(0, 1, 3, 2).reshape(g * 512, n)


def relu(v):
    return np.maximum(v, 0.0)


K, T, E, C, H, N = 1024, 384, 12, 128, 512, 256
TOP = 4


def by_expert(wq, xq):
    return np.concatenate([wq[e].T @ xq[:, e * C:(e + 1) * C] for e in range(E)], axis=1)


def setup_inputs():
    n = np.random.standard_normal
    s = mx_kscale(K)[:, None]
    u = mx_kscale(H)
    deal = np.repeat(np.arange(E), C).reshape(TOP, T)[:, np.random.permutation(T)]
    deal = np.take_along_axis(deal, np.argsort(np.random.rand(TOP, T), axis=0), axis=0)
    for _ in range(8):
        s_, t_ = np.random.permutation(T).reshape(2, -1); r = np.random.randint(TOP, size=T // 2); x, y = deal[r, s_].copy(), deal[r, t_].copy()
        ok = ~((deal[:, s_] == y).any(0) | (deal[:, t_] == x).any(0)); deal[r[ok], s_[ok]] = y[ok]; deal[r[ok], t_[ok]] = x[ok]
    order = np.lexsort((np.random.rand(TOP * T), deal.reshape(-1)))
    slot_token = order % T; pos = np.empty(TOP * T, np.int64); pos[order] = np.arange(TOP * T); pos = pos.reshape(TOP, T)
    g = np.random.uniform(0.5, 1.5, (TOP, T)); g = g / g.sum(0)
    w1 = [pack_weight(m, "e2m1") for m in n((E, K, H)) / np.sqrt(K) / s[None] * u[None, None, :]]
    w2 = [pack_weight(m, "e2m1") for m in n((E, H, N)) / np.sqrt(H) / u[None, :, None]]
    return {
        "xT": (n((K, T)) * s).astype(np.float32),
        "w1_words": np.stack([m[0] for m in w1]),
        "w1_scales": np.stack([m[1] for m in w1]),
        "w2_words": np.stack([m[0] for m in w2]),
        "w2_scales": np.stack([m[1] for m in w2]),
        "gate": np.stack([np.tile(r, (N, 1)) for r in g]).astype(np.float32),
        "offs": striped(slot_token),
        "pos1": striped(pos[0]),
        "pos2": striped(pos[1]),
        "pos3": striped(pos[2]),
        "pos4": striped(pos[3]),
    }


def reference(xT, w1_words, w1_scales, w2_words, w2_scales, gate, offs, pos1, pos2, pos3, pos4):
    idx = unstriped(offs)
    w1 = np.stack([unpack_weight(w1_words[e], w1_scales[e], "e2m1") for e in range(E)])
    w2 = np.stack([unpack_weight(w2_words[e], w2_scales[e], "e2m1") for e in range(E)])
    xq = mxq(f64(xT)[:, idx], 0, "e4m3")
    h = relu(by_expert(w1, xq))
    y = by_expert(w2, mxq(h, 0, "e4m3"))
    return sum(f64(gate[r]) * y[:, unstriped(p)] for r, p in enumerate((pos1, pos2, pos3, pos4)))

@@ -1,0 +1,288 @@
+from contextlib import ExitStack
+
+import concourse.mybir as mybir
+from concourse.masks import make_identity
+
+F32 = mybir.dt.float32
+BF16 = mybir.dt.bfloat16
+I32 = mybir.dt.int32
+U32 = mybir.dt.uint32
+U16 = mybir.dt.uint16
+U8 = mybir.dt.uint8
+FP8X4 = mybir.dt.float8_e4m3fn_x4
+FP4X4 = mybir.dt.float4_e2m1fn_x4
+MULT = mybir.AluOpType.mult
+RELU = mybir.ActivationFunctionType.Relu
+
+K, T, E, C, H, N, TOP = 1024, 384, 12, 128, 512, 256, 4
+P = 128
+PASSES = K // 512
+WINDOW = 512
+FLOPS = 2 * TOP * T * (K * H + H * N)
+
+
+def tile_moe_tk_mlp_relu_kernel(
+    tc, xT, w1_words, w1_scales, w2_words, w2_scales, gate, offs, pos1, pos2, pos3, pos4, out
+):
+    nc = tc.nc
+    with ExitStack() as ctx:
+        keep = ctx.enter_context(tc.tile_pool(name="keep", bufs=1))
+        words_pool = []
+        for s in range(PASSES):
+            words_pool.append(ctx.enter_context(tc.tile_pool(name=f"words_pool{s}", bufs=(2, 2)[s])))
+        bytes_pool = []
+        for s in range(PASSES):
+            bytes_pool.append(ctx.enter_context(tc.tile_pool(name=f"bytes_pool{s}", bufs=2)))
+        psum_a = ctx.enter_context(tc.psum_pool(name="psum_a", bufs=4))
+        psum_t = ctx.enter_context(tc.psum_pool(name="psum_t", bufs=2))
+        psum_y = ctx.enter_context(tc.psum_pool(name="psum_y", bufs=2))
+
+        w1_words32 = w1_words.bitcast(I32)
+        w1_scales32 = w1_scales.bitcast(I32)
+        w2_words32 = w2_words.bitcast(I32)
+        w2_scales32 = w2_scales.bitcast(I32)
+        raw = []
+        w1_at = {}
+        w1s_at = {}
+        w2_at = {}
+
+        def load_x(s):
+            r = keep.tile([P, 4, T], F32, name=f"raw{s}")
+            nc.sync.dma_start(out=r[:], in_=xT[512 * s : 512 * (s + 1), :].rearrange("(p j) w -> p j w", j=4))
+            raw.append(r)
+
+        def load_w1(a):
+            w = keep.tile([P, 2, PASSES, 2 * H], U8, name=f"w1w{a}", align_bytes=64)
+            nc.sync.dma_start(
+                out=w[:].rearrange("p e s w -> p (e s) w").bitcast(I32),
+                in_=w1_words32[a : a + 2].rearrange("e s p w -> p (e s) w"),
+            )
+            for e in range(2):
+                w1_at[a + e] = w[:, e]
+
+        def load_w1_scales(a, b, zero):
+            sc = keep.tile([P, b - a, PASSES, H], U8, name=f"w1s{a}", align_bytes=64)
+            zero.memset(sc[:].rearrange("p e s i -> p (e s i)").bitcast(I32), 0)
+            for q in range(4):
+                nc.sync.dma_start(
+                    out=sc[32 * q : 32 * q + 4].rearrange("p e s i -> p (e s) i").bitcast(I32),
+                    in_=w1_scales32[a:b, :, 4 * q : 4 * q + 4, :].rearrange("e s q i -> q (e s) i"),
+                )
+            for e in range(a, b):
+                w1s_at[e] = sc[:, e - a]
+
+        def load_w2(a, b):
+            w = keep.tile([P, b - a, 2 * N], U8, name=f"w2w{a}", align_bytes=64)
+            nc.sync.dma_start(out=w[:].bitcast(I32), in_=w2_words32[a:b, 0].rearrange("e p w -> p e w"))
+            for e in range(a, b):
+                w2_at[e] = w[:, e - a]
+
+        warm = keep.tile([P, 1], F32, name="warm")
+        nc.gpsimd.memset(warm[:], 0.0)
+        warm_out = keep.tile([P, 1], F32, name="warm_out")
+        nc.scalar.activation(warm_out[:], warm[:], RELU)
+        ident = keep.tile([P, P], F32, name="ident")
+        make_identity(nc, ident[:])
+        load_x(0)
+        load_x(1)
+        offs_t = keep.tile([P, TOP * T // 16], U16, name="offs_t")
+        nc.sync.dma_start(offs_t[:], offs)
+        load_w1(0)
+        load_w1_scales(0, 4, nc.vector)
+        load_w1(2)
+        load_w1(4)
+        load_w1_scales(4, E, nc.gpsimd)
+        w2s = keep.tile([P, E, N], U8, name="w2s", align_bytes=64)
+        nc.gpsimd.memset(w2s[:].rearrange("p e n -> p (e n)").bitcast(I32), 0)
+        for q in range(4):
+            nc.sync.dma_start(
+                out=w2s[32 * q : 32 * q + 4].bitcast(I32),
+                in_=w2_scales32[:, 0, 4 * q : 4 * q + 4, :].rearrange("e q n -> q e n"),
+            )
+        load_w2(0, 4)
+        load_w1(6)
+        load_w1(8)
+        load_w2(4, E)
+        load_w1(10)
+        gate_t = []
+        for h in range(2):
+            g = keep.tile([P, TOP, T], F32, name=f"gate_t{h}")
+            nc.sync.dma_start(out=g[:], in_=gate[:, P * h : P * (h + 1), :].rearrange("r p t -> p r t"))
+            gate_t.append(g)
+        pos_t = []
+        for r, pos in enumerate((pos1, pos2, pos3, pos4)):
+            pt = keep.tile([P, T // 16], U16, name=f"pos_t{r}")
+            nc.sync.dma_start(pt[:], pos)
+            pos_t.append(pt)
+        x_bytes = []
+        for s in range(PASSES):
+            b = keep.tile([P, WINDOW], U8, name=f"x_bytes{s}", align_bytes=64)
+            nc.vector.memset(b[:].bitcast(I32), 0)
+            x_bytes.append(b)
+
+        x_words = []
+        for s in range(PASSES):
+            w = keep.tile([P, WINDOW], I32, name=f"x_words{s}", align_bytes=64)
+            nc.vector.memset(w[:, T:], 0)
+            x_words.append(w)
+
+        def quantise_tokens(s, cut):
+            xb = keep.tile([P, T, 4], BF16, name=f"xb{s}", align_bytes=64)
+            nc.vector.tensor_copy(out=xb[:, :cut, :], in_=raw[s][:, :, :cut].rearrange("p j w -> p w j"))
+            nc.scalar.copy(out=xb[:, cut:, :], in_=raw[s][:, :, cut:].rearrange("p j w -> p w j"))
+            for cols in (slice(0, 256), slice(256, T)):
+                nc.vector.quantize_mx(
+                    out=x_words[s][:, cols].bitcast(FP8X4),
+                    scales=x_bytes[s][:, cols],
+                    in_=xb[:, cols, :].rearrange("p w j -> p (w j)"),
+                )
+
+        y_t = []
+        for h in range(2):
+            y = keep.tile([P, TOP * T], F32, name=f"y_t{h}")
+            y_t.append(y)
+
+        bytes_at = {}
+        words_at = {}
+        acc_at = {}
+        act_at = {}
+        turned_at = {}
+        ready_at = {}
+        hidden_at = {}
+        yp_at = {}
+
+        def gather_bytes(s, a, b):
+            gb = bytes_pool[s].tile([P, C * (b - a)], U8, name=f"bytes{s}", align_bytes=64)
+            nc.vector.tensor_copy(gb[:], x_bytes[s][:].indirect(offs_t[:, C // 16 * a : C // 16 * b]))
+            for e in range(a, b):
+                bytes_at[e, s] = gb[:, C * (e - a) : C * (e - a + 1)]
+
+        def gather_words(s, a, b):
+            gw = words_pool[s].tile([P, C * (b - a)], U32, name=f"words{s}", align_bytes=64)
+            nc.vector.tensor_copy(gw[:], x_words[s][:].bitcast(U32).indirect(offs_t[:, C // 16 * a : C // 16 * b]))
+            for e in range(a, b):
+                words_at[e, s] = gw[:, C * (e - a) : C * (e - a + 1)]
+
+        def first_product(e, s):
+            if s == 0:
+                acc_at[e] = psum_a.tile([P, H], F32, name="acc")
+            nc.tensor.matmul_mx(
+                out=acc_at[e][:],
+                lhsT=words_at[e, s].bitcast(FP8X4),
+                lhsT_scale=bytes_at[e, s],
+                rhs=w1_at[e][:, s, :].bitcast(FP4X4),
+                rhs_scale=w1s_at[e][:, s, :],
+                start=(s == 0),
+                stop=(s == PASSES - 1),
+            )
+
+        def relu(e):
+            act = keep.tile([P, H], BF16, name=f"act{e}")
+            nc.scalar.activation(
+                act[:].rearrange("p (u m d) -> p u m d", u=2, d=2),
+                acc_at[e][:].rearrange("p (m u d) -> p u m d", u=2, d=2),
+                RELU,
+            )
+            act_at[e] = act
+
+        def turn(e, a, b):
+            if e == a:
+                turned_at[a] = psum_t.tile([P, 2, 2, C], F32, name="tp")
+            for u in range(2):
+                nc.tensor.transpose(
+                    turned_at[a][:, e - a, u, :], act_at[e][:].bitcast(F32)[:, C * u : C * (u + 1)], ident[:]
+                )
+
+        def interleave(copy, a, b):
+            ht = keep.tile([P, (b - a) * C * 4], BF16, name=f"ht{a}", align_bytes=64)
+            copy(
+                out=ht[:].bitcast(F32).rearrange("p (i r u) -> p i r u", i=b - a, u=2),
+                in_=turned_at[a][:, : b - a].rearrange("p i u r -> p i r u"),
+            )
+            ready_at[a] = ht
+
+        def quantise_hidden(a, b):
+            hw = keep.tile([P, (b - a) * C], U32, name=f"hw{a}", align_bytes=64)
+            hb = keep.tile([P, (b - a) * C], U8, name=f"hb{a}", align_bytes=64)
+            nc.vector.quantize_mx(out=hw[:].bitcast(FP8X4), scales=hb[:], in_=ready_at[a][:])
+            for e in range(a, b):
+                cols = slice(C * (e - a), C * (e - a + 1))
+                hidden_at[e] = (hw[:, cols], hb[:, cols])
+
+        def second_product(e):
+            if e % 2 == 0:
+                yp_at[e // 2] = psum_y.tile([P, 2, 2 * C], F32, name="yp")
+            hw, hb = hidden_at[e]
+            for h in range(2):
+                nc.tensor.matmul_mx(
+                    out=yp_at[e // 2][:, h, C * (e % 2) : C * (e % 2 + 1)],
+                    lhsT=w2_at[e][:, 2 * P * h : 2 * P * (h + 1)].bitcast(FP4X4),
+                    lhsT_scale=w2s[:, e, P * h : P * (h + 1)],
+                    rhs=hw.bitcast(FP8X4),
+                    rhs_scale=hb,
+                    start=True,
+                    stop=True,
+                )
+
+        def keep_y(copy, e, h):
+            copy(out=y_t[h][:, C * e : C * (e + 2)], in_=yp_at[e // 2][:, h, :])
+
+        on_scalar = nc.scalar.copy
+        on_vector = nc.vector.tensor_copy
+        quantise_tokens(0, 256)
+        gather_bytes(0, 0, 2)
+        gather_words(0, 0, 2)
+        quantise_tokens(1, 128)
+        gather_bytes(1, 0, 2)
+        gather_words(1, 0, 2)
+        plan = []
+        for e in range(2, E, 2):
+            for s in range(PASSES):
+                plan.append((e - 2 + 0.02 * s, gather_bytes, (s, e, e + 2)))
+                plan.append((e - 2 + 0.03 * s, gather_words, (s, e, e + 2)))
+        for e in range(E):
+            plan.append((e - 1.5, first_product, (e, 0)))
+            plan.append((e + 0.1, first_product, (e, 1)))
+            plan.append((e + 0.2, relu, (e,)))
+        for a, b in ((0, 2), (2, 4), (4, 6), (6, 8), (8, 10), (10, 11), (11, 12)):
+            for e in range(a, b):
+                plan.append((b - 1 + 2 + 0.3, turn, (e, a, b)))
+                plan.append((b - 1 + 3 + 1.5 + 0.6, second_product, (e,)))
+            plan.append((b - 1 + 2.5 + 0.4, interleave, (on_vector if 99 <= a < 99 else on_scalar, a, b)))
+            plan.append((b - 1 + 3 + 0.5, quantise_hidden, (a, b)))
+        for e in range(0, E, 2):
+            for h in range(2):
+                plan.append((e + 1 + 3 + 2 + 0.7, keep_y, (on_vector if h == 1 and e >= 99 else on_scalar, e, h)))
+        for when, step, what in sorted(plan, key=lambda entry: entry[0]):
+            step(*what)
+
+        z = []
+        part = []
+        o = []
+        for h in range(2):
+            zt = keep.tile([P, TOP, T], F32, name=f"z{h}")
+            pt = keep.tile([P, 2, T], F32, name=f"part{h}")
+            ot = keep.tile([P, T], F32, name=f"o{h}")
+            z.append(zt)
+            part.append(pt)
+            o.append(ot)
+
+        def fetch(h, r):
+            nc.vector.tensor_tensor(z[h][:, r, :], y_t[h][:].indirect(pos_t[r][:]), gate_t[h][:, r, :], MULT)
+
+        def store(h):
+            nc.sync.dma_start(out=out[P * h : P * (h + 1), :], in_=o[h][:])
+
+        for r in range(TOP):
+            fetch(0, r)
+        fetch(1, 0)
+        fetch(1, 1)
+        nc.vector.tensor_add(part[0][:], z[0][:, 0:2, :], z[0][:, 2:4, :])
+        fetch(1, 2)
+        nc.vector.tensor_add(part[1][:, 0, :], z[1][:, 0, :], z[1][:, 1, :])
+        nc.vector.tensor_add(o[0][:], part[0][:, 0, :], part[0][:, 1, :])
+        store(0)
+        nc.vector.tensor_add(part[1][:, 1, :], part[1][:, 0, :], z[1][:, 2, :])
+        fetch(1, 3)
+        nc.vector.tensor_add(o[1][:], part[1][:, 1, :], z[1][:, 3, :])
+        store(1)

@@ -63,10 +63,10 @@ def tile_moe_tk_mlp_relu_kernel(
         def load_w1_scales(a, b, zero):
             sc = keep.tile([P, b - a, PASSES, H], U8, name=f"w1s{a}", align_bytes=64)
             zero.memset(sc[:].rearrange("p e s i -> p (e s i)").bitcast(I32), 0)
-            for q in range(4):
+            for r in range(4):
                 nc.sync.dma_start(
-                    out=sc[32 * q : 32 * q + 4].rearrange("p e s i -> p (e s) i").bitcast(I32),
-                    in_=w1_scales32[a:b, :, 4 * q : 4 * q + 4, :].rearrange("e s q i -> q (e s) i"),
+                    out=sc[r:P:32].rearrange("p e s i -> p (e s) i").bitcast(I32),
+                    in_=w1_scales32[a:b, :, r:16:4, :].rearrange("e s q i -> q (e s) i"),
                 )
             for e in range(a, b):
                 w1s_at[e] = sc[:, e - a]
@@ -94,21 +94,19 @@ def tile_moe_tk_mlp_relu_kernel(
         load_w1_scales(4, E, nc.gpsimd)
         w2s = keep.tile([P, E, N], U8, name="w2s", align_bytes=64)
         nc.gpsimd.memset(w2s[:].rearrange("p e n -> p (e n)").bitcast(I32), 0)
-        for q in range(4):
+        for r in range(4):
             nc.sync.dma_start(
-                out=w2s[32 * q : 32 * q + 4].bitcast(I32),
-                in_=w2_scales32[:, 0, 4 * q : 4 * q + 4, :].rearrange("e q n -> q e n"),
+                out=w2s[r:P:32].bitcast(I32),
+                in_=w2_scales32[:, 0, r:16:4, :].rearrange("e q n -> q e n"),
             )
         load_w2(0, 4)
         load_w1(6)
         load_w1(8)
         load_w2(4, E)
         load_w1(10)
-        gate_t = []
-        for h in range(2):
-            g = keep.tile([P, TOP, T], F32, name=f"gate_t{h}")
-            nc.sync.dma_start(out=g[:], in_=gate[:, P * h : P * (h + 1), :].rearrange("r p t -> p r t"))
-            gate_t.append(g)
+        g = keep.tile([P, TOP, T], F32, name="gate_t")
+        nc.sync.dma_start(out=g[:], in_=gate[:, 0:P, :].rearrange("r p t -> p r t"))
+        gate_t = [g, g]
         pos_t = []
         for r, pos in enumerate((pos1, pos2, pos3, pos4)):
             pt = keep.tile([P, T // 16], U16, name=f"pos_t{r}")

@@ -13,11 +13,13 @@ FP8X4 = mybir.dt.float8_e4m3fn_x4
 FP4X4 = mybir.dt.float4_e2m1fn_x4
 MULT = mybir.AluOpType.mult
 RELU = mybir.ActivationFunctionType.Relu
+COPY = mybir.ActivationFunctionType.Copy
 
 K, T, E, C, H, N, TOP = 1024, 384, 12, 128, 512, 256, 4
 P = 128
 PASSES = K // 512
 WINDOW = 512
+BYTE_WINDOW = 704
 FLOPS = 2 * TOP * T * (K * H + H * N)
 
 
@@ -27,15 +29,10 @@ def tile_moe_tk_mlp_relu_kernel(
     nc = tc.nc
     with ExitStack() as ctx:
         keep = ctx.enter_context(tc.tile_pool(name="keep", bufs=1))
-        words_pool = []
-        for s in range(PASSES):
-            words_pool.append(ctx.enter_context(tc.tile_pool(name=f"words_pool{s}", bufs=(2, 2)[s])))
-        bytes_pool = []
-        for s in range(PASSES):
-            bytes_pool.append(ctx.enter_context(tc.tile_pool(name=f"bytes_pool{s}", bufs=2)))
-        psum_a = ctx.enter_context(tc.psum_pool(name="psum_a", bufs=4))
-        psum_t = ctx.enter_context(tc.psum_pool(name="psum_t", bufs=2))
-        psum_y = ctx.enter_context(tc.psum_pool(name="psum_y", bufs=2))
+        psum = ctx.enter_context(tc.psum_pool(name="psum", bufs=1))
+
+        def bank(n, shape):
+            return psum.tile(shape, F32, name=f"bank{n}")
 
         w1_words32 = w1_words.bitcast(I32)
         w1_scales32 = w1_scales.bitcast(I32)
@@ -60,9 +57,12 @@ def tile_moe_tk_mlp_relu_kernel(
             for e in range(2):
                 w1_at[a + e] = w[:, e]
 
-        def load_w1_scales(a, b, zero):
+        def load_w1_scales(a, b, cut):
             sc = keep.tile([P, b - a, PASSES, H], U8, name=f"w1s{a}", align_bytes=64)
-            zero.memset(sc[:].rearrange("p e s i -> p (e s i)").bitcast(I32), 0)
+            flat = sc[:].rearrange("p e s i -> p (e s i)").bitcast(I32)
+            nc.vector.memset(flat[:, :cut], 0)
+            if cut < (b - a) * PASSES * H // 4:
+                nc.gpsimd.memset(flat[:, cut:], 0)
             for r in range(4):
                 nc.sync.dma_start(
                     out=sc[r:P:32].rearrange("p e s i -> p (e s) i").bitcast(I32),
@@ -77,47 +77,51 @@ def tile_moe_tk_mlp_relu_kernel(
             for e in range(a, b):
                 w2_at[e] = w[:, e - a]
 
-        warm = keep.tile([P, 1], F32, name="warm")
-        nc.gpsimd.memset(warm[:], 0.0)
-        warm_out = keep.tile([P, 1], F32, name="warm_out")
-        nc.scalar.activation(warm_out[:], warm[:], RELU)
         ident = keep.tile([P, P], F32, name="ident")
         make_identity(nc, ident[:])
+
         load_x(0)
         load_x(1)
         offs_t = keep.tile([P, TOP * T // 16], U16, name="offs_t")
         nc.sync.dma_start(offs_t[:], offs)
         load_w1(0)
-        load_w1_scales(0, 4, nc.vector)
-        load_w1(2)
-        load_w1(4)
-        load_w1_scales(4, E, nc.gpsimd)
+        load_w1_scales(0, 4, 1024)
         w2s = keep.tile([P, E, N], U8, name="w2s", align_bytes=64)
-        nc.gpsimd.memset(w2s[:].rearrange("p e n -> p (e n)").bitcast(I32), 0)
-        for r in range(4):
-            nc.sync.dma_start(
-                out=w2s[r:P:32].bitcast(I32),
-                in_=w2_scales32[:, 0, r:16:4, :].rearrange("e q n -> q e n"),
-            )
-        load_w2(0, 4)
-        load_w1(6)
-        load_w1(8)
-        load_w2(4, E)
-        load_w1(10)
-        g = keep.tile([P, TOP, T], F32, name="gate_t")
-        nc.sync.dma_start(out=g[:], in_=gate[:, 0:P, :].rearrange("r p t -> p r t"))
-        gate_t = [g, g]
         pos_t = []
-        for r, pos in enumerate((pos1, pos2, pos3, pos4)):
-            pt = keep.tile([P, T // 16], U16, name=f"pos_t{r}")
-            nc.sync.dma_start(pt[:], pos)
-            pos_t.append(pt)
-        x_bytes = []
-        for s in range(PASSES):
-            b = keep.tile([P, WINDOW], U8, name=f"x_bytes{s}", align_bytes=64)
-            nc.vector.memset(b[:].bitcast(I32), 0)
-            x_bytes.append(b)
+        gate_t = []
 
+        def second_loads():
+            load_w1(2)
+            load_w1_scales(4, E, 768)
+            load_w1(4)
+            load_w1(6)
+
+        def third_loads():
+            nc.vector.memset(w2s[:].rearrange("p e n -> p (e n)").bitcast(I32), 0)
+            for r in range(4):
+                nc.sync.dma_start(
+                    out=w2s[r:P:32].bitcast(I32),
+                    in_=w2_scales32[:, 0, r:16:4, :].rearrange("e q n -> q e n"),
+                )
+            load_w2(0, 4)
+            load_w1(8)
+            load_w1(10)
+
+        def last_loads():
+            load_w2(4, E)
+            for r, pos in enumerate((pos1, pos2, pos3, pos4)):
+                pt = keep.tile([P, T // 16], U16, name=f"pos_t{r}")
+                nc.sync.dma_start(pt[:], pos)
+                pos_t.append(pt)
+            for r in range(TOP):
+                g = keep.tile([P, T], F32, name=f"gate_t{r}")
+                nc.sync.dma_start(out=g[:], in_=gate[r, 0:P, :])
+                gate_t.append(g)
+
+        x_bytes = keep.tile([P, BYTE_WINDOW], U8, name="x_bytes", align_bytes=64)
+        nc.vector.memset(x_bytes[:].bitcast(I32), 0)
+        moved = keep.tile([P, E * C], U8, name="moved", align_bytes=64)
+        nc.vector.memset(moved[:].bitcast(I32), 0)
         x_words = []
         for s in range(PASSES):
             w = keep.tile([P, WINDOW], I32, name=f"x_words{s}", align_bytes=64)
@@ -126,94 +130,95 @@ def tile_moe_tk_mlp_relu_kernel(
 
         def quantise_tokens(s, cut):
             xb = keep.tile([P, T, 4], BF16, name=f"xb{s}", align_bytes=64)
-            nc.vector.tensor_copy(out=xb[:, :cut, :], in_=raw[s][:, :, :cut].rearrange("p j w -> p w j"))
-            nc.scalar.copy(out=xb[:, cut:, :], in_=raw[s][:, :, cut:].rearrange("p j w -> p w j"))
+            if cut:
+                nc.vector.tensor_copy(out=xb[:, :cut, :], in_=raw[s][:, :, :cut].rearrange("p j w -> p w j"))
+            nc.scalar.activation(xb[:, cut:, :], raw[s][:, :, cut:].rearrange("p j w -> p w j"), COPY)
             for cols in (slice(0, 256), slice(256, T)):
                 nc.vector.quantize_mx(
                     out=x_words[s][:, cols].bitcast(FP8X4),
-                    scales=x_bytes[s][:, cols],
+                    scales=x_bytes[4 * (1 - s) : P, cols],
                     in_=xb[:, cols, :].rearrange("p w j -> p (w j)"),
                 )
 
-        y_t = []
-        for h in range(2):
-            y = keep.tile([P, TOP * T], F32, name=f"y_t{h}")
-            y_t.append(y)
-
+        y_t = [keep.tile([P, TOP * T], F32, name=f"y_t{h}") for h in range(2)]
         bytes_at = {}
         words_at = {}
-        acc_at = {}
         act_at = {}
-        turned_at = {}
-        ready_at = {}
         hidden_at = {}
-        yp_at = {}
 
-        def gather_bytes(s, a, b):
-            gb = bytes_pool[s].tile([P, C * (b - a)], U8, name=f"bytes{s}", align_bytes=64)
-            nc.vector.tensor_copy(gb[:], x_bytes[s][:].indirect(offs_t[:, C // 16 * a : C // 16 * b]))
+        def gather_bytes(a, b, name):
+            gb = keep.tile([P, C * (b - a)], U8, name=name, align_bytes=64)
+            nc.vector.tensor_copy(gb[:], x_bytes[:].indirect(offs_t[:, C // 16 * a : C // 16 * b]))
             for e in range(a, b):
-                bytes_at[e, s] = gb[:, C * (e - a) : C * (e - a + 1)]
+                bytes_at[e, 1] = gb[:, C * (e - a) : C * (e - a + 1)]
+            return gb
 
-        def gather_words(s, a, b):
-            gw = words_pool[s].tile([P, C * (b - a)], U32, name=f"words{s}", align_bytes=64)
-            nc.vector.tensor_copy(gw[:], x_words[s][:].bitcast(U32).indirect(offs_t[:, C // 16 * a : C // 16 * b]))
+        def move_bytes(a, b, gb):
+            for r in range(4):
+                nc.sync.dma_start(
+                    out=moved[r:P:32, C * a : C * b].bitcast(I32),
+                    in_=gb[4 + r : P : 32, :].bitcast(I32),
+                )
+            for e in range(a, b):
+                bytes_at[e, 0] = moved[:, C * e : C * (e + 1)]
+
+        def gather_words(s, a, b, gw):
+            nc.vector.tensor_copy(gw, x_words[s][:].bitcast(U32).indirect(offs_t[:, C // 16 * a : C // 16 * b]))
             for e in range(a, b):
                 words_at[e, s] = gw[:, C * (e - a) : C * (e - a + 1)]
 
-        def first_product(e, s):
-            if s == 0:
-                acc_at[e] = psum_a.tile([P, H], F32, name="acc")
-            nc.tensor.matmul_mx(
-                out=acc_at[e][:],
-                lhsT=words_at[e, s].bitcast(FP8X4),
-                lhsT_scale=bytes_at[e, s],
-                rhs=w1_at[e][:, s, :].bitcast(FP4X4),
-                rhs_scale=w1s_at[e][:, s, :],
-                start=(s == 0),
-                stop=(s == PASSES - 1),
-            )
+        def words_tile(n, name):
+            return keep.tile([P, n * C], U32, name=name, align_bytes=64)
 
-        def relu(e):
+        def first_product(e):
+            acc = bank(e % 4, [P, H])
+            for s in range(PASSES):
+                nc.tensor.matmul_mx(
+                    out=acc[:],
+                    lhsT=words_at[e, s].bitcast(FP8X4),
+                    lhsT_scale=bytes_at[e, s],
+                    rhs=w1_at[e][:, s, :].bitcast(FP4X4),
+                    rhs_scale=w1s_at[e][:, s, :],
+                    start=(s == 0),
+                    stop=(s == PASSES - 1),
+                )
             act = keep.tile([P, H], BF16, name=f"act{e}")
             nc.scalar.activation(
                 act[:].rearrange("p (u m d) -> p u m d", u=2, d=2),
-                acc_at[e][:].rearrange("p (m u d) -> p u m d", u=2, d=2),
+                acc[:].rearrange("p (m u d) -> p u m d", u=2, d=2),
                 RELU,
             )
             act_at[e] = act
 
-        def turn(e, a, b):
-            if e == a:
-                turned_at[a] = psum_t.tile([P, 2, 2, C], F32, name="tp")
-            for u in range(2):
-                nc.tensor.transpose(
-                    turned_at[a][:, e - a, u, :], act_at[e][:].bitcast(F32)[:, C * u : C * (u + 1)], ident[:]
-                )
-
-        def interleave(copy, a, b):
-            ht = keep.tile([P, (b - a) * C * 4], BF16, name=f"ht{a}", align_bytes=64)
+        def turn(a, b, n, ht, copy=nc.scalar.copy):
+            turned = bank(n, [P, b - a, 2, C])
+            for e in range(a, b):
+                for u in range(2):
+                    nc.tensor.transpose(
+                        turned[:, e - a, u, :], act_at[e][:].bitcast(F32)[:, C * u : C * (u + 1)], ident[:]
+                    )
             copy(
-                out=ht[:].bitcast(F32).rearrange("p (i r u) -> p i r u", i=b - a, u=2),
-                in_=turned_at[a][:, : b - a].rearrange("p i u r -> p i r u"),
+                out=ht.bitcast(F32).rearrange("p (i r u) -> p i r u", i=b - a, u=2),
+                in_=turned[:].rearrange("p i u r -> p i r u"),
             )
-            ready_at[a] = ht
 
-        def quantise_hidden(a, b):
-            hw = keep.tile([P, (b - a) * C], U32, name=f"hw{a}", align_bytes=64)
+        def hidden_tile(a, b):
+            return keep.tile([P, (b - a) * H], BF16, name=f"ht{a}", align_bytes=64)
+
+        def quantise_hidden(a, b, ht, slot=None):
+            hw = keep.tile([P, (b - a) * C], U32, name=slot or f"hw{a}", align_bytes=64)
             hb = keep.tile([P, (b - a) * C], U8, name=f"hb{a}", align_bytes=64)
-            nc.vector.quantize_mx(out=hw[:].bitcast(FP8X4), scales=hb[:], in_=ready_at[a][:])
+            nc.vector.quantize_mx(out=hw[:].bitcast(FP8X4), scales=hb[:], in_=ht[:])
             for e in range(a, b):
                 cols = slice(C * (e - a), C * (e - a + 1))
                 hidden_at[e] = (hw[:, cols], hb[:, cols])
 
-        def second_product(e):
-            if e % 2 == 0:
-                yp_at[e // 2] = psum_y.tile([P, 2, 2 * C], F32, name="yp")
-            hw, hb = hidden_at[e]
-            for h in range(2):
+        def second_product(h, a, b, n, copy=nc.scalar.copy):
+            yp = bank(n, [P, (b - a) * C])
+            for e in range(a, b):
+                hw, hb = hidden_at[e]
                 nc.tensor.matmul_mx(
-                    out=yp_at[e // 2][:, h, C * (e % 2) : C * (e % 2 + 1)],
+                    out=yp[:, C * (e - a) : C * (e - a + 1)],
                     lhsT=w2_at[e][:, 2 * P * h : 2 * P * (h + 1)].bitcast(FP4X4),
                     lhsT_scale=w2s[:, e, P * h : P * (h + 1)],
                     rhs=hw.bitcast(FP8X4),
@@ -221,66 +226,75 @@ def tile_moe_tk_mlp_relu_kernel(
                     start=True,
                     stop=True,
                 )
-
-        def keep_y(copy, e, h):
-            copy(out=y_t[h][:, C * e : C * (e + 2)], in_=yp_at[e // 2][:, h, :])
+            copy(out=y_t[h][:, C * a : C * b], in_=yp[:])
 
         on_scalar = nc.scalar.copy
         on_vector = nc.vector.tensor_copy
-        quantise_tokens(0, 256)
-        gather_bytes(0, 0, 2)
-        gather_words(0, 0, 2)
-        quantise_tokens(1, 128)
-        gather_bytes(1, 0, 2)
-        gather_words(1, 0, 2)
-        plan = []
-        for e in range(2, E, 2):
-            for s in range(PASSES):
-                plan.append((e - 2 + 0.02 * s, gather_bytes, (s, e, e + 2)))
-                plan.append((e - 2 + 0.03 * s, gather_words, (s, e, e + 2)))
-        for e in range(E):
-            plan.append((e - 1.5, first_product, (e, 0)))
-            plan.append((e + 0.1, first_product, (e, 1)))
-            plan.append((e + 0.2, relu, (e,)))
-        for a, b in ((0, 2), (2, 4), (4, 6), (6, 8), (8, 10), (10, 11), (11, 12)):
-            for e in range(a, b):
-                plan.append((b - 1 + 2 + 0.3, turn, (e, a, b)))
-                plan.append((b - 1 + 3 + 1.5 + 0.6, second_product, (e,)))
-            plan.append((b - 1 + 2.5 + 0.4, interleave, (on_vector if 99 <= a < 99 else on_scalar, a, b)))
-            plan.append((b - 1 + 3 + 0.5, quantise_hidden, (a, b)))
-        for e in range(0, E, 2):
-            for h in range(2):
-                plan.append((e + 1 + 3 + 2 + 0.7, keep_y, (on_vector if h == 1 and e >= 99 else on_scalar, e, h)))
-        for when, step, what in sorted(plan, key=lambda entry: entry[0]):
-            step(*what)
+        quantise_tokens(0, 224)
+        move_bytes(0, 4, gather_bytes(0, 4, "bytes_early"))
+        second_loads()
+        gather_words(0, 0, 2, words_tile(2, "early")[:])
+        quantise_tokens(1, 0)
+        late = words_tile(E - 2, "xb1")
+        second = words_tile(E, "second")
 
-        z = []
-        part = []
-        o = []
+        def gather_pair(a):
+            gather_words(0, a, a + 2, late[:, C * (a - 2) : C * a])
+            gather_words(1, a, a + 2, second[:, C * a : C * (a + 2)])
+
+        gather_bytes(0, 2, "bytes0")
+        gather_words(1, 0, 2, second[:, : 2 * C])
+        gather_bytes(2, 4, "bytes2")
+        gather_pair(2)
+        move_bytes(4, 8, gather_bytes(4, 8, "bytes4"))
+        third_loads()
+        gather_pair(4)
+        gather_pair(6)
+        move_bytes(8, E, gather_bytes(8, E, "bytes8"))
+        last_loads()
+        gather_words(0, 8, 10, late[:, 6 * C : 8 * C])
+        gather_words(0, 10, 12, late[:, 8 * C :])
+        gather_words(1, 10, 11, second[:, 10 * C : 11 * C])
+
+        for e in range(4):
+            first_product(e)
+        for a in (0, 2):
+            ht = hidden_tile(a, a + 2)
+            turn(a, a + 2, 5 - a // 2, ht[:])
+            quantise_hidden(a, a + 2, ht)
+        gather_words(1, 8, 10, words_tile(2, "ht0")[:])
+        gather_words(1, 11, 12, words_tile(1, "ht2")[:])
+        for e in range(4, 8):
+            first_product(e)
+        middle = hidden_tile(4, 8)
+        for a in (4, 6):
+            turn(a, a + 2, 7 - a // 2, middle[:, H * (a - 4) : H * (a - 2)])
+        second_product(0, 0, 4, 6, on_vector)
+        for e in range(8, E):
+            first_product(e)
+        quantise_hidden(4, 8, middle, "ht2")
+        for a, b, n, copy in ((8, 10, 0, on_vector), (10, 11, 4, on_scalar), (11, 12, 5, on_scalar)):
+            ht = hidden_tile(a, b)
+            turn(a, b, n, ht[:], copy)
+            quantise_hidden(a, b, ht)
+        second_product(0, 4, 8, 7)
+        second_product(0, 8, 11, 6, on_vector)
+        second_product(0, 11, 12, 1)
+        second_product(1, 8, 12, 5)
+        second_product(1, 0, 4, 1)
+        second_product(1, 4, 8, 5)
+
         for h in range(2):
-            zt = keep.tile([P, TOP, T], F32, name=f"z{h}")
-            pt = keep.tile([P, 2, T], F32, name=f"part{h}")
-            ot = keep.tile([P, T], F32, name=f"o{h}")
-            z.append(zt)
-            part.append(pt)
-            o.append(ot)
-
-        def fetch(h, r):
-            nc.vector.tensor_tensor(z[h][:, r, :], y_t[h][:].indirect(pos_t[r][:]), gate_t[h][:, r, :], MULT)
-
-        def store(h):
-            nc.sync.dma_start(out=out[P * h : P * (h + 1), :], in_=o[h][:])
-
-        for r in range(TOP):
-            fetch(0, r)
-        fetch(1, 0)
-        fetch(1, 1)
-        nc.vector.tensor_add(part[0][:], z[0][:, 0:2, :], z[0][:, 2:4, :])
-        fetch(1, 2)
-        nc.vector.tensor_add(part[1][:, 0, :], z[1][:, 0, :], z[1][:, 1, :])
-        nc.vector.tensor_add(o[0][:], part[0][:, 0, :], part[0][:, 1, :])
-        store(0)
-        nc.vector.tensor_add(part[1][:, 1, :], part[1][:, 0, :], z[1][:, 2, :])
-        fetch(1, 3)
-        nc.vector.tensor_add(o[1][:], part[1][:, 1, :], z[1][:, 3, :])
-        store(1)
+            z = keep.tile([P, TOP, T], F32, name=f"z{h}")
+            total = keep.tile([P, TOP - 1, T], F32, name=f"total{h}")
+            for r in range(TOP):
+                nc.vector.tensor_tensor(z[:, r, :], y_t[h][:].indirect(pos_t[r][:]), gate_t[r][:], MULT)
+                if r == 2 and h == 1:
+                    nc.vector.tensor_add(total[:, 0, :], z[:, 0, :], z[:, 1, :])
+                    nc.vector.tensor_add(total[:, 1, :], total[:, 0, :], z[:, 2, :])
+            if h == 0:
+                nc.vector.tensor_add(total[:, 0:2, :], z[:, 0:2, :], z[:, 2:4, :])
+                nc.vector.tensor_add(total[:, 2, :], total[:, 0, :], total[:, 1, :])
+            else:
+                nc.vector.tensor_add(total[:, 2, :], total[:, 1, :], z[:, 3, :])
+            nc.sync.dma_start(out=out[P * h : P * (h + 1), :], in_=total[:, 2, :])

@@ -19,7 +19,6 @@ K, T, E, C, H, N, TOP = 1024, 384, 12, 128, 512, 256, 4
 P = 128
 PASSES = K // 512
 WINDOW = 512
-BYTE_WINDOW = 704
 FLOPS = 2 * TOP * T * (K * H + H * N)
 
 
@@ -44,7 +43,7 @@ def tile_moe_tk_mlp_relu_kernel(
         w2_at = {}
 
         def load_x(s):
-            r = keep.tile([P, 4, T], F32, name=f"raw{s}")
+            r = keep.tile([P, 4, T], F32, name=f"raw{s}", align_bytes=64)
             nc.sync.dma_start(out=r[:], in_=xT[512 * s : 512 * (s + 1), :].rearrange("(p j) w -> p j w", j=4))
             raw.append(r)
 
@@ -57,12 +56,9 @@ def tile_moe_tk_mlp_relu_kernel(
             for e in range(2):
                 w1_at[a + e] = w[:, e]
 
-        def load_w1_scales(a, b, cut):
+        def load_w1_scales(a, b, zero):
             sc = keep.tile([P, b - a, PASSES, H], U8, name=f"w1s{a}", align_bytes=64)
-            flat = sc[:].rearrange("p e s i -> p (e s i)").bitcast(I32)
-            nc.vector.memset(flat[:, :cut], 0)
-            if cut < (b - a) * PASSES * H // 4:
-                nc.gpsimd.memset(flat[:, cut:], 0)
+            zero.memset(sc[:].rearrange("p e s i -> p (e s i)").bitcast(I32), 0)
             for r in range(4):
                 nc.sync.dma_start(
                     out=sc[r:P:32].rearrange("p e s i -> p (e s) i").bitcast(I32),
@@ -84,46 +80,37 @@ def tile_moe_tk_mlp_relu_kernel(
         load_x(1)
         offs_t = keep.tile([P, TOP * T // 16], U16, name="offs_t")
         nc.sync.dma_start(offs_t[:], offs)
-        load_w1(0)
-        load_w1_scales(0, 4, 1024)
+        load_w1_scales(0, 4, nc.vector)
+        load_w1_scales(4, 8, nc.gpsimd)
+        load_w1_scales(8, E, nc.vector)
         w2s = keep.tile([P, E, N], U8, name="w2s", align_bytes=64)
+        nc.vector.memset(w2s[:].rearrange("p e n -> p (e n)").bitcast(I32), 0)
+        for r in range(4):
+            nc.sync.dma_start(
+                out=w2s[r:P:32].bitcast(I32),
+                in_=w2_scales32[:, 0, r:16:4, :].rearrange("e q n -> q e n"),
+            )
+        for a in range(0, E, 2):
+            load_w1(a)
+        load_w2(0, 8)
+        load_w2(8, E)
         pos_t = []
         gate_t = []
+        for r, pos in enumerate((pos1, pos2, pos3, pos4)):
+            pt = keep.tile([P, T // 16], U16, name=f"pos_t{r}")
+            nc.sync.dma_start(pt[:], pos)
+            pos_t.append(pt)
+        for r in range(TOP):
+            g = keep.tile([P, T], F32, name=f"gate_t{r}")
+            nc.sync.dma_start(out=g[:], in_=gate[r, 0:P, :])
+            gate_t.append(g)
 
-        def second_loads():
-            load_w1(2)
-            load_w1_scales(4, E, 768)
-            load_w1(4)
-            load_w1(6)
-
-        def third_loads():
-            nc.vector.memset(w2s[:].rearrange("p e n -> p (e n)").bitcast(I32), 0)
-            for r in range(4):
-                nc.sync.dma_start(
-                    out=w2s[r:P:32].bitcast(I32),
-                    in_=w2_scales32[:, 0, r:16:4, :].rearrange("e q n -> q e n"),
-                )
-            load_w2(0, 4)
-            load_w1(8)
-            load_w1(10)
-
-        def last_loads():
-            load_w2(4, E)
-            for r, pos in enumerate((pos1, pos2, pos3, pos4)):
-                pt = keep.tile([P, T // 16], U16, name=f"pos_t{r}")
-                nc.sync.dma_start(pt[:], pos)
-                pos_t.append(pt)
-            for r in range(TOP):
-                g = keep.tile([P, T], F32, name=f"gate_t{r}")
-                nc.sync.dma_start(out=g[:], in_=gate[r, 0:P, :])
-                gate_t.append(g)
-
-        x_bytes = keep.tile([P, BYTE_WINDOW], U8, name="x_bytes", align_bytes=64)
-        nc.vector.memset(x_bytes[:].bitcast(I32), 0)
-        moved = keep.tile([P, E * C], U8, name="moved", align_bytes=64)
-        nc.vector.memset(moved[:].bitcast(I32), 0)
+        x_bytes = []
         x_words = []
         for s in range(PASSES):
+            b = keep.tile([P, WINDOW], U8, name=f"x_bytes{s}", align_bytes=64)
+            nc.vector.memset(b[:].bitcast(I32), 0)
+            x_bytes.append(b)
             w = keep.tile([P, WINDOW], I32, name=f"x_words{s}", align_bytes=64)
             nc.vector.memset(w[:, T:], 0)
             x_words.append(w)
@@ -136,7 +123,7 @@ def tile_moe_tk_mlp_relu_kernel(
             for cols in (slice(0, 256), slice(256, T)):
                 nc.vector.quantize_mx(
                     out=x_words[s][:, cols].bitcast(FP8X4),
-                    scales=x_bytes[4 * (1 - s) : P, cols],
+                    scales=x_bytes[s][:, cols],
                     in_=xb[:, cols, :].rearrange("p w j -> p (w j)"),
                 )
 
@@ -146,21 +133,13 @@ def tile_moe_tk_mlp_relu_kernel(
         act_at = {}
         hidden_at = {}
 
-        def gather_bytes(a, b, name):
-            gb = keep.tile([P, C * (b - a)], U8, name=name, align_bytes=64)
-            nc.vector.tensor_copy(gb[:], x_bytes[:].indirect(offs_t[:, C // 16 * a : C // 16 * b]))
+        def gather_bytes(s, a, b, gb):
+            nc.vector.tensor_copy(gb, x_bytes[s][:].indirect(offs_t[:, C // 16 * a : C // 16 * b]))
             for e in range(a, b):
-                bytes_at[e, 1] = gb[:, C * (e - a) : C * (e - a + 1)]
-            return gb
+                bytes_at[e, s] = gb[:, C * (e - a) : C * (e - a + 1)]
 
-        def move_bytes(a, b, gb):
-            for r in range(4):
-                nc.sync.dma_start(
-                    out=moved[r:P:32, C * a : C * b].bitcast(I32),
-                    in_=gb[4 + r : P : 32, :].bitcast(I32),
-                )
-            for e in range(a, b):
-                bytes_at[e, 0] = moved[:, C * e : C * (e + 1)]
+        def bytes_tile(n, name):
+            return keep.tile([P, n * C], U8, name=name, align_bytes=64)
 
         def gather_words(s, a, b, gw):
             nc.vector.tensor_copy(gw, x_words[s][:].bitcast(U32).indirect(offs_t[:, C // 16 * a : C // 16 * b]))
@@ -205,8 +184,8 @@ def tile_moe_tk_mlp_relu_kernel(
         def hidden_tile(a, b):
             return keep.tile([P, (b - a) * H], BF16, name=f"ht{a}", align_bytes=64)
 
-        def quantise_hidden(a, b, ht, slot=None):
-            hw = keep.tile([P, (b - a) * C], U32, name=slot or f"hw{a}", align_bytes=64)
+        def quantise_hidden(a, b, ht):
+            hw = keep.tile([P, (b - a) * C], U32, name=f"hw{a}", align_bytes=64)
             hb = keep.tile([P, (b - a) * C], U8, name=f"hb{a}", align_bytes=64)
             nc.vector.quantize_mx(out=hw[:].bitcast(FP8X4), scales=hb[:], in_=ht[:])
             for e in range(a, b):
@@ -230,56 +209,50 @@ def tile_moe_tk_mlp_relu_kernel(
 
         on_scalar = nc.scalar.copy
         on_vector = nc.vector.tensor_copy
-        quantise_tokens(0, 224)
-        move_bytes(0, 4, gather_bytes(0, 4, "bytes_early"))
-        second_loads()
-        gather_words(0, 0, 2, words_tile(2, "early")[:])
+        quantise_tokens(0, 208)
+        gather_bytes(0, 0, 3, bytes_tile(3, "early_bytes")[:])
+        gather_words(0, 0, 3, words_tile(3, "early_words")[:])
         quantise_tokens(1, 0)
-        late = words_tile(E - 2, "xb1")
-        second = words_tile(E, "second")
+        late_bytes = bytes_tile(E - 3, "raw1")
+        late_words = words_tile(E - 3, "xb1")
+        second_bytes = bytes_tile(E, "second_bytes")
+        second_words = words_tile(E, "second_words")
+        quads = [hidden_tile(0, 4), hidden_tile(4, 8)]
 
-        def gather_pair(a):
-            gather_words(0, a, a + 2, late[:, C * (a - 2) : C * a])
-            gather_words(1, a, a + 2, second[:, C * a : C * (a + 2)])
+        def both_bytes(a, b):
+            gather_bytes(0, a, b, late_bytes[:, C * (a - 3) : C * (b - 3)])
+            gather_bytes(1, a, b, second_bytes[:, C * a : C * b])
 
-        gather_bytes(0, 2, "bytes0")
-        gather_words(1, 0, 2, second[:, : 2 * C])
-        gather_bytes(2, 4, "bytes2")
-        gather_pair(2)
-        move_bytes(4, 8, gather_bytes(4, 8, "bytes4"))
-        third_loads()
-        gather_pair(4)
-        gather_pair(6)
-        move_bytes(8, E, gather_bytes(8, E, "bytes8"))
-        last_loads()
-        gather_words(0, 8, 10, late[:, 6 * C : 8 * C])
-        gather_words(0, 10, 12, late[:, 8 * C :])
-        gather_words(1, 10, 11, second[:, 10 * C : 11 * C])
+        def both_words(a, b):
+            gather_words(0, a, b, late_words[:, C * (a - 3) : C * (b - 3)])
+            gather_words(1, a, b, second_words[:, C * a : C * b])
 
-        for e in range(4):
-            first_product(e)
-        for a in (0, 2):
-            ht = hidden_tile(a, a + 2)
-            turn(a, a + 2, 5 - a // 2, ht[:])
-            quantise_hidden(a, a + 2, ht)
-        gather_words(1, 8, 10, words_tile(2, "ht0")[:])
-        gather_words(1, 11, 12, words_tile(1, "ht2")[:])
-        for e in range(4, 8):
-            first_product(e)
-        middle = hidden_tile(4, 8)
-        for a in (4, 6):
-            turn(a, a + 2, 7 - a // 2, middle[:, H * (a - 4) : H * (a - 2)])
-        second_product(0, 0, 4, 6, on_vector)
-        for e in range(8, E):
-            first_product(e)
-        quantise_hidden(4, 8, middle, "ht2")
+        gather_bytes(1, 0, 3, second_bytes[:, : 3 * C])
+        gather_words(1, 0, 3, second_words[:, : 3 * C])
+        both_bytes(3, 6)
+        both_words(3, 6)
+        both_bytes(6, 9)
+        both_words(6, 8)
+        both_bytes(9, E)
+        both_words(8, 10)
+        gather_words(0, 10, E, late_words[:, C * 7 :])
+        for e in (10, 11):
+            gather_words(1, e, e + 1, second_words[:, C * e : C * (e + 1)])
+        for a in range(0, E, 2):
+            first_product(a)
+            first_product(a + 1)
+            if 2 <= a <= 8:
+                first = (a - 2) % 4
+                turn(a - 2, a, 4 + a // 2 % 2, quads[(a - 2) // 4][:, H * first : H * (first + 2)])
+        quantise_hidden(0, 4, quads[0])
+        quantise_hidden(4, 8, quads[1])
         for a, b, n, copy in ((8, 10, 0, on_vector), (10, 11, 4, on_scalar), (11, 12, 5, on_scalar)):
             ht = hidden_tile(a, b)
             turn(a, b, n, ht[:], copy)
             quantise_hidden(a, b, ht)
-        second_product(0, 4, 8, 7)
-        second_product(0, 8, 11, 6, on_vector)
-        second_product(0, 11, 12, 1)
+        second_product(0, 0, 4, 6)
+        second_product(0, 4, 8, 7, on_vector)
+        second_product(0, 8, 12, 1)
         second_product(1, 8, 12, 5)
         second_product(1, 0, 4, 1)
         second_product(1, 4, 8, 5)

@@ -77,9 +77,9 @@ def tile_moe_tk_mlp_relu_kernel(
         make_identity(nc, ident[:])
 
         load_x(0)
-        load_x(1)
         offs_t = keep.tile([P, TOP * T // 16], U16, name="offs_t")
         nc.sync.dma_start(offs_t[:], offs)
+        load_x(1)
         load_w1_scales(0, 4, nc.vector)
         load_w1_scales(4, 8, nc.gpsimd)
         load_w1_scales(8, E, nc.vector)
@@ -210,32 +210,34 @@ def tile_moe_tk_mlp_relu_kernel(
         on_scalar = nc.scalar.copy
         on_vector = nc.vector.tensor_copy
         quantise_tokens(0, 208)
-        gather_bytes(0, 0, 3, bytes_tile(3, "early_bytes")[:])
-        gather_words(0, 0, 3, words_tile(3, "early_words")[:])
+        early_bytes = bytes_tile(4, "early_bytes")
+        early_words = words_tile(4, "early_words")
+        for a in (0, 2):
+            gather_bytes(0, a, a + 2, early_bytes[:, C * a : C * (a + 2)])
+            gather_words(0, a, a + 2, early_words[:, C * a : C * (a + 2)])
         quantise_tokens(1, 0)
-        late_bytes = bytes_tile(E - 3, "raw1")
-        late_words = words_tile(E - 3, "xb1")
+        late_bytes = bytes_tile(E - 4, "raw1")
+        late_words = words_tile(E - 4, "xb1")
         second_bytes = bytes_tile(E, "second_bytes")
         second_words = words_tile(E, "second_words")
         quads = [hidden_tile(0, 4), hidden_tile(4, 8)]
 
-        def both_bytes(a, b):
-            gather_bytes(0, a, b, late_bytes[:, C * (a - 3) : C * (b - 3)])
-            gather_bytes(1, a, b, second_bytes[:, C * a : C * b])
+        def first_pass(a, b):
+            gather_bytes(0, a, b, late_bytes[:, C * (a - 4) : C * (b - 4)])
+            gather_words(0, a, b, late_words[:, C * (a - 4) : C * (b - 4)])
 
-        def both_words(a, b):
-            gather_words(0, a, b, late_words[:, C * (a - 3) : C * (b - 3)])
+        def second_pass(a, b):
+            gather_bytes(1, a, b, second_bytes[:, C * a : C * b])
             gather_words(1, a, b, second_words[:, C * a : C * b])
 
-        gather_bytes(1, 0, 3, second_bytes[:, : 3 * C])
-        gather_words(1, 0, 3, second_words[:, : 3 * C])
-        both_bytes(3, 6)
-        both_words(3, 6)
-        both_bytes(6, 9)
-        both_words(6, 8)
-        both_bytes(9, E)
-        both_words(8, 10)
-        gather_words(0, 10, E, late_words[:, C * 7 :])
+        second_pass(0, 3)
+        first_pass(4, 7)
+        second_pass(3, 6)
+        first_pass(7, 10)
+        second_pass(6, 8)
+        second_pass(8, 10)
+        first_pass(10, E)
+        gather_bytes(1, 10, E, second_bytes[:, C * 10 :])
         for e in (10, 11):
             gather_words(1, e, e + 1, second_words[:, C * e : C * (e + 1)])
         for a in range(0, E, 2):
@@ -257,17 +259,33 @@ def tile_moe_tk_mlp_relu_kernel(
         second_product(1, 0, 4, 1)
         second_product(1, 4, 8, 5)
 
+        def fetch(h, r, name):
+            z = keep.tile([P, T], F32, name=name)
+            nc.vector.tensor_tensor(z[:], y_t[h][:].indirect(pos_t[r][:]), gate_t[r][:], MULT)
+            return z
+
+        partial = []
         for h in range(2):
-            z = keep.tile([P, TOP, T], F32, name=f"z{h}")
-            total = keep.tile([P, TOP - 1, T], F32, name=f"total{h}")
-            for r in range(TOP):
-                nc.vector.tensor_tensor(z[:, r, :], y_t[h][:].indirect(pos_t[r][:]), gate_t[r][:], MULT)
-                if r == 2 and h == 1:
-                    nc.vector.tensor_add(total[:, 0, :], z[:, 0, :], z[:, 1, :])
-                    nc.vector.tensor_add(total[:, 1, :], total[:, 0, :], z[:, 2, :])
-            if h == 0:
-                nc.vector.tensor_add(total[:, 0:2, :], z[:, 0:2, :], z[:, 2:4, :])
-                nc.vector.tensor_add(total[:, 2, :], total[:, 0, :], total[:, 1, :])
-            else:
-                nc.vector.tensor_add(total[:, 2, :], total[:, 1, :], z[:, 3, :])
-            nc.sync.dma_start(out=out[P * h : P * (h + 1), :], in_=total[:, 2, :])
+            acc = [bank(n, [P, C]) for n in ((0, 2, 6), (7, 1, 5))[h]]
+            for r in range(TOP - 1):
+                z = fetch(h, r, f"z{h}{r}")
+                for b in range(3):
+                    nc.tensor.matmul(
+                        acc[b][:],
+                        lhsT=z[:, C * b : C * (b + 1)],
+                        rhs=ident[:],
+                        is_transpose=True,
+                        start=(r == 0),
+                        stop=(r == TOP - 2),
+                    )
+            summed = keep.tile([P, 3, C], F32, name=f"summed{h}")
+            back = bank(3 + h, [P, T])
+            for b in range(3):
+                nc.scalar.copy(out=summed[:, b, :], in_=acc[b][:])
+                nc.tensor.transpose(back[:, C * b : C * (b + 1)], summed[:, b, :], ident[:])
+            partial.append(back)
+        last = [fetch(0, TOP - 1, "z11"), fetch(1, TOP - 1, "z13")]
+        for h in range(2):
+            total = keep.tile([P, T], F32, name=f"total{h}")
+            nc.vector.tensor_add(total[:], last[h][:], partial[h][:])
+            nc.sync.dma_start(out=out[P * h : P * (h + 1), :], in_=total[:])

@@ -117,10 +117,17 @@ def tile_moe_tk_mlp_relu_kernel(
 
         def quantise_tokens(s, cut):
             xb = keep.tile([P, T, 4], BF16, name=f"xb{s}", align_bytes=64)
-            if cut:
-                nc.vector.tensor_copy(out=xb[:, :cut, :], in_=raw[s][:, :, :cut].rearrange("p j w -> p w j"))
-            nc.scalar.activation(xb[:, cut:, :], raw[s][:, :, cut:].rearrange("p j w -> p w j"), COPY)
-            for cols in (slice(0, 256), slice(256, T)):
+            for a, b in ((0, C), (C, cut)) if cut else ():
+                nc.vector.tensor_copy(
+                    out=xb[:, a:b, :].rearrange("p (c i) j -> p c j i", i=4),
+                    in_=raw[s][:, :, a:b].rearrange("p j (c i) -> p c j i", i=4),
+                )
+            nc.scalar.activation(
+                xb[:, cut:, :].rearrange("p (c i) j -> p c j i", i=4),
+                raw[s][:, :, cut:].rearrange("p j (c i) -> p c j i", i=4),
+                COPY,
+            )
+            for cols in (slice(0, C), slice(C, T)):
                 nc.vector.quantize_mx(
                     out=x_words[s][:, cols].bitcast(FP8X4),
                     scales=x_bytes[s][:, cols],
@@ -254,38 +261,53 @@ def tile_moe_tk_mlp_relu_kernel(
             quantise_hidden(a, b, ht)
         second_product(0, 0, 4, 6)
         second_product(0, 4, 8, 7, on_vector)
-        second_product(0, 8, 12, 1)
+        second_product(0, 8, 10, 1)
+        second_product(0, 10, 12, 3)
         second_product(1, 8, 12, 5)
         second_product(1, 0, 4, 1)
         second_product(1, 4, 8, 5)
 
-        def fetch(h, r, name):
-            z = keep.tile([P, T], F32, name=name)
-            nc.vector.tensor_tensor(z[:], y_t[h][:].indirect(pos_t[r][:]), gate_t[r][:], MULT)
-            return z
+        def fetch(h, r, z, cols):
+            nc.vector.tensor_tensor(
+                z[:, cols],
+                y_t[h][:].indirect(pos_t[r][:, cols.start // 16 : cols.stop // 16]),
+                gate_t[r][:, cols],
+                MULT,
+            )
 
-        partial = []
-        for h in range(2):
-            acc = [bank(n, [P, C]) for n in ((0, 2, 6), (7, 1, 5))[h]]
-            for r in range(TOP - 1):
-                z = fetch(h, r, f"z{h}{r}")
+        blocks = [slice(C * b, C * (b + 1)) for b in range(3)]
+
+        def summed_on_tensor(h, terms, back):
+            acc = [bank(n, [P, C]) for n in (0, 2, 6)]
+            for r in range(terms):
+                z = keep.tile([P, T], F32, name=f"z{h}{r}")
+                for cols in blocks if (h, r) == (1, terms - 1) else [slice(0, T)]:
+                    fetch(h, r, z, cols)
                 for b in range(3):
                     nc.tensor.matmul(
                         acc[b][:],
-                        lhsT=z[:, C * b : C * (b + 1)],
+                        lhsT=z[:, blocks[b]],
                         rhs=ident[:],
                         is_transpose=True,
                         start=(r == 0),
-                        stop=(r == TOP - 2),
+                        stop=(r == terms - 1),
                     )
             summed = keep.tile([P, 3, C], F32, name=f"summed{h}")
-            back = bank(3 + h, [P, T])
             for b in range(3):
                 nc.scalar.copy(out=summed[:, b, :], in_=acc[b][:])
-                nc.tensor.transpose(back[:, C * b : C * (b + 1)], summed[:, b, :], ident[:])
-            partial.append(back)
-        last = [fetch(0, TOP - 1, "z11"), fetch(1, TOP - 1, "z13")]
-        for h in range(2):
-            total = keep.tile([P, T], F32, name=f"total{h}")
-            nc.vector.tensor_add(total[:], last[h][:], partial[h][:])
-            nc.sync.dma_start(out=out[P * h : P * (h + 1), :], in_=total[:])
+                nc.tensor.transpose(back[b], summed[:, b, :], ident[:])
+
+        total = [keep.tile([P, T], F32, name=f"total{h}") for h in range(2)]
+        back = bank(4, [P, T])
+        summed_on_tensor(0, TOP, [back[:, cols] for cols in blocks])
+        nc.scalar.copy(out=total[0][:], in_=back[:])
+        nc.sync.dma_start(out=out[0:P, :], in_=total[0][:])
+        pieces = (slice(0, 2 * C), slice(2 * C, T))
+        backs = [bank(7, [P, 2 * C]), bank(3, [P, C])]
+        summed_on_tensor(1, TOP - 1, [backs[0][:, :C], backs[0][:, C:], backs[1][:]])
+        last = keep.tile([P, T], F32, name="last")
+        for cols in pieces:
+            fetch(1, TOP - 1, last, cols)
+        for b, cols in enumerate(pieces):
+            nc.vector.tensor_add(total[1][:, cols], last[:, cols], backs[b][:])
+            nc.sync.dma_start(out=out[P:, cols], in_=total[1][:, cols])

@@ -66,6 +66,7 @@ def tile_moe_tk_mlp_relu_kernel(
                 )
             for e in range(a, b):
                 w1s_at[e] = sc[:, e - a]
+            return sc
 
         def load_w2(a, b):
             w = keep.tile([P, b - a, 2 * N], U8, name=f"w2w{a}", align_bytes=64)
@@ -80,30 +81,18 @@ def tile_moe_tk_mlp_relu_kernel(
         offs_t = keep.tile([P, TOP * T // 16], U16, name="offs_t")
         nc.sync.dma_start(offs_t[:], offs)
         load_x(1)
-        load_w1_scales(0, 4, nc.vector)
-        load_w1_scales(4, 8, nc.gpsimd)
+        first_plane = load_w1_scales(0, 4, nc.vector)
+        load_w1_scales(4, 8, nc.vector)
         load_w1_scales(8, E, nc.vector)
-        w2s = keep.tile([P, E, N], U8, name="w2s", align_bytes=64)
-        nc.vector.memset(w2s[:].rearrange("p e n -> p (e n)").bitcast(I32), 0)
-        for r in range(4):
-            nc.sync.dma_start(
-                out=w2s[r:P:32].bitcast(I32),
-                in_=w2_scales32[:, 0, r:16:4, :].rearrange("e q n -> q e n"),
-            )
         for a in range(0, E, 2):
             load_w1(a)
         load_w2(0, 8)
         load_w2(8, E)
         pos_t = []
-        gate_t = []
         for r, pos in enumerate((pos1, pos2, pos3, pos4)):
             pt = keep.tile([P, T // 16], U16, name=f"pos_t{r}")
             nc.sync.dma_start(pt[:], pos)
             pos_t.append(pt)
-        for r in range(TOP):
-            g = keep.tile([P, T], F32, name=f"gate_t{r}")
-            nc.sync.dma_start(out=g[:], in_=gate[r, 0:P, :])
-            gate_t.append(g)
 
         x_bytes = []
         x_words = []
@@ -216,7 +205,7 @@ def tile_moe_tk_mlp_relu_kernel(
 
         on_scalar = nc.scalar.copy
         on_vector = nc.vector.tensor_copy
-        quantise_tokens(0, 208)
+        quantise_tokens(0, 256)
         early_bytes = bytes_tile(4, "early_bytes")
         early_words = words_tile(4, "early_words")
         for a in (0, 2):
@@ -253,6 +242,14 @@ def tile_moe_tk_mlp_relu_kernel(
             if 2 <= a <= 8:
                 first = (a - 2) % 4
                 turn(a - 2, a, 4 + a // 2 % 2, quads[(a - 2) // 4][:, H * first : H * (first + 2)])
+        w2s = first_plane[:].rearrange("p e s i -> p (e s i)")[:, : E * N].rearrange("p (e n) -> p e n", n=N)
+        for r in range(4):
+            nc.sync.dma_start(
+                out=w2s[r:P:32].bitcast(I32),
+                in_=w2_scales32[:, 0, r:16:4, :].rearrange("e q n -> q e n"),
+            )
+        gate_t = keep.tile([P, TOP, T], F32, name="w1s4", align_bytes=64)
+        nc.sync.dma_start(out=gate_t[:], in_=gate[:, 0:P, :].rearrange("r p t -> p r t"))
         quantise_hidden(0, 4, quads[0])
         quantise_hidden(4, 8, quads[1])
         for a, b, n, copy in ((8, 10, 0, on_vector), (10, 11, 4, on_scalar), (11, 12, 5, on_scalar)):
@@ -271,7 +268,7 @@ def tile_moe_tk_mlp_relu_kernel(
             nc.vector.tensor_tensor(
                 z[:, cols],
                 y_t[h][:].indirect(pos_t[r][:, cols.start // 16 : cols.stop // 16]),
-                gate_t[r][:, cols],
+                gate_t[:, r, cols],
                 MULT,
             )
 

@@ -19,6 +19,7 @@ K, T, E, C, H, N, TOP = 1024, 384, 12, 128, 512, 256, 4
 P = 128
 PASSES = K // 512
 WINDOW = 512
+EARLY = 5
 FLOPS = 2 * TOP * T * (K * H + H * N)
 
 
@@ -81,10 +82,11 @@ def tile_moe_tk_mlp_relu_kernel(
         offs_t = keep.tile([P, TOP * T // 16], U16, name="offs_t")
         nc.sync.dma_start(offs_t[:], offs)
         load_x(1)
+        load_w1(0)
         first_plane = load_w1_scales(0, 4, nc.vector)
         load_w1_scales(4, 8, nc.vector)
         load_w1_scales(8, E, nc.vector)
-        for a in range(0, E, 2):
+        for a in range(2, E, 2):
             load_w1(a)
         load_w2(0, 8)
         load_w2(8, E)
@@ -94,15 +96,12 @@ def tile_moe_tk_mlp_relu_kernel(
             nc.sync.dma_start(pt[:], pos)
             pos_t.append(pt)
 
-        x_bytes = []
-        x_words = []
-        for s in range(PASSES):
-            b = keep.tile([P, WINDOW], U8, name=f"x_bytes{s}", align_bytes=64)
-            nc.vector.memset(b[:].bitcast(I32), 0)
-            x_bytes.append(b)
-            w = keep.tile([P, WINDOW], I32, name=f"x_words{s}", align_bytes=64)
-            nc.vector.memset(w[:, T:], 0)
-            x_words.append(w)
+        all_bytes = keep.tile([P, T + WINDOW], U8, name="all_bytes", align_bytes=64)
+        all_words = keep.tile([P, T + WINDOW], I32, name="all_words", align_bytes=64)
+        nc.vector.memset(all_bytes[:, 2 * T :].bitcast(I32), 0)
+        nc.vector.memset(all_words[:, 2 * T :], 0)
+        x_bytes = [all_bytes[:, T:], all_bytes[:, :WINDOW]]
+        x_words = [all_words[:, T:], all_words[:, :WINDOW]]
 
         def quantise_tokens(s, cut):
             xb = keep.tile([P, T, 4], BF16, name=f"xb{s}", align_bytes=64)
@@ -130,7 +129,7 @@ def tile_moe_tk_mlp_relu_kernel(
         hidden_at = {}
 
         def gather_bytes(s, a, b, gb):
-            nc.vector.tensor_copy(gb, x_bytes[s][:].indirect(offs_t[:, C // 16 * a : C // 16 * b]))
+            nc.vector.tensor_copy(gb, x_bytes[s].indirect(offs_t[:, C // 16 * a : C // 16 * b]))
             for e in range(a, b):
                 bytes_at[e, s] = gb[:, C * (e - a) : C * (e - a + 1)]
 
@@ -138,7 +137,7 @@ def tile_moe_tk_mlp_relu_kernel(
             return keep.tile([P, n * C], U8, name=name, align_bytes=64)
 
         def gather_words(s, a, b, gw):
-            nc.vector.tensor_copy(gw, x_words[s][:].bitcast(U32).indirect(offs_t[:, C // 16 * a : C // 16 * b]))
+            nc.vector.tensor_copy(gw, x_words[s].bitcast(U32).indirect(offs_t[:, C // 16 * a : C // 16 * b]))
             for e in range(a, b):
                 words_at[e, s] = gw[:, C * (e - a) : C * (e - a + 1)]
 
@@ -205,33 +204,32 @@ def tile_moe_tk_mlp_relu_kernel(
 
         on_scalar = nc.scalar.copy
         on_vector = nc.vector.tensor_copy
-        quantise_tokens(0, 256)
-        early_bytes = bytes_tile(4, "early_bytes")
-        early_words = words_tile(4, "early_words")
-        for a in (0, 2):
-            gather_bytes(0, a, a + 2, early_bytes[:, C * a : C * (a + 2)])
-            gather_words(0, a, a + 2, early_words[:, C * a : C * (a + 2)])
+        quantise_tokens(0, 288)
+        early_bytes = bytes_tile(EARLY, "early_bytes")
+        early_words = words_tile(EARLY, "early_words")
+        for a, b in ((0, 2), (2, EARLY)):
+            gather_bytes(0, a, b, early_bytes[:, C * a : C * b])
+            gather_words(0, a, b, early_words[:, C * a : C * b])
         quantise_tokens(1, 0)
-        late_bytes = bytes_tile(E - 4, "raw1")
-        late_words = words_tile(E - 4, "xb1")
+        late_bytes = bytes_tile(E - EARLY, "raw1")
+        late_words = words_tile(E - EARLY, "xb1")
         second_bytes = bytes_tile(E, "second_bytes")
         second_words = words_tile(E, "second_words")
         quads = [hidden_tile(0, 4), hidden_tile(4, 8)]
 
         def first_pass(a, b):
-            gather_bytes(0, a, b, late_bytes[:, C * (a - 4) : C * (b - 4)])
-            gather_words(0, a, b, late_words[:, C * (a - 4) : C * (b - 4)])
+            gather_bytes(0, a, b, late_bytes[:, C * (a - EARLY) : C * (b - EARLY)])
+            gather_words(0, a, b, late_words[:, C * (a - EARLY) : C * (b - EARLY)])
 
         def second_pass(a, b):
             gather_bytes(1, a, b, second_bytes[:, C * a : C * b])
             gather_words(1, a, b, second_words[:, C * a : C * b])
 
-        second_pass(0, 3)
-        first_pass(4, 7)
-        second_pass(3, 6)
-        first_pass(7, 10)
-        second_pass(6, 8)
-        second_pass(8, 10)
+        second_pass(0, 2)
+        second_pass(2, EARLY)
+        for a, b in ((EARLY, 8), (8, 10)):
+            first_pass(a, b)
+            second_pass(a, b)
         first_pass(10, E)
         gather_bytes(1, 10, E, second_bytes[:, C * 10 :])
         for e in (10, 11):

@@ -246,7 +246,7 @@ def tile_moe_tk_mlp_relu_kernel(
                 out=w2s[r:P:32].bitcast(I32),
                 in_=w2_scales32[:, 0, r:16:4, :].rearrange("e q n -> q e n"),
             )
-        gate_t = keep.tile([P, TOP, T], F32, name="w1s4", align_bytes=64)
+        gate_t = keep.tile([P, TOP, T], F32, name="gate_t", align_bytes=64)
         nc.sync.dma_start(out=gate_t[:], in_=gate[:, 0:P, :].rearrange("r p t -> p r t"))
         quantise_hidden(0, 4, quads[0])
         quantise_hidden(4, 8, quads[1])

@@ -19,7 +19,8 @@ K, T, E, C, H, N, TOP = 1024, 384, 12, 128, 512, 256, 4
 P = 128
 PASSES = K // 512
 WINDOW = 512
-EARLY = 5
+EARLY = 6
+ROWS = (2, 4)
 FLOPS = 2 * TOP * T * (K * H + H * N)
 
 
@@ -29,6 +30,7 @@ def tile_moe_tk_mlp_relu_kernel(
     nc = tc.nc
     with ExitStack() as ctx:
         keep = ctx.enter_context(tc.tile_pool(name="keep", bufs=1))
+        shared = ctx.enter_context(tc.tile_pool(name="shared", bufs=1))
         psum = ctx.enter_context(tc.psum_pool(name="psum", bufs=1))
 
         def bank(n, shape):
@@ -44,9 +46,13 @@ def tile_moe_tk_mlp_relu_kernel(
         w2_at = {}
 
         def load_x(s):
-            r = keep.tile([P, 4, T], F32, name=f"raw{s}", align_bytes=64)
-            nc.sync.dma_start(out=r[:], in_=xT[512 * s : 512 * (s + 1), :].rearrange("(p j) w -> p j w", j=4))
-            raw.append(r)
+            rows = xT[512 * s : 512 * (s + 1), :].rearrange("(p j) w -> p j w", j=4)
+            parts = []
+            for j in range(0, 4, ROWS[s]):
+                r = keep.tile([P, ROWS[s], T], F32, name=f"raw{s}{j}", align_bytes=64)
+                nc.sync.dma_start(out=r[:], in_=rows[:, j : j + ROWS[s], :])
+                parts.append((slice(j, j + ROWS[s]), r))
+            raw.append(parts)
 
         def load_w1(a):
             w = keep.tile([P, 2, PASSES, 2 * H], U8, name=f"w1w{a}", align_bytes=64)
@@ -56,10 +62,12 @@ def tile_moe_tk_mlp_relu_kernel(
             )
             for e in range(2):
                 w1_at[a + e] = w[:, e]
+            return w
 
-        def load_w1_scales(a, b, zero):
-            sc = keep.tile([P, b - a, PASSES, H], U8, name=f"w1s{a}", align_bytes=64)
-            zero.memset(sc[:].rearrange("p e s i -> p (e s i)").bitcast(I32), 0)
+        def load_w1_scales(a, b, sc=None):
+            if sc is None:
+                sc = keep.tile([P, b - a, PASSES, H], U8, name=f"w1s{a}", align_bytes=64)
+                nc.vector.memset(sc[:].rearrange("p e s i -> p (e s i)").bitcast(I32), 0)
             for r in range(4):
                 nc.sync.dma_start(
                     out=sc[r:P:32].rearrange("p e s i -> p (e s) i").bitcast(I32),
@@ -82,39 +90,33 @@ def tile_moe_tk_mlp_relu_kernel(
         offs_t = keep.tile([P, TOP * T // 16], U16, name="offs_t")
         nc.sync.dma_start(offs_t[:], offs)
         load_x(1)
-        load_w1(0)
-        first_plane = load_w1_scales(0, 4, nc.vector)
-        load_w1_scales(4, 8, nc.vector)
-        load_w1_scales(8, E, nc.vector)
-        for a in range(2, E, 2):
+        first_words = load_w1(0)
+        load_w1(2)
+        first_plane = load_w1_scales(0, 4)
+        load_w1_scales(4, 8)
+        for a in range(4, 8, 2):
             load_w1(a)
-        load_w2(0, 8)
-        load_w2(8, E)
-        pos_t = []
-        for r, pos in enumerate((pos1, pos2, pos3, pos4)):
-            pt = keep.tile([P, T // 16], U16, name=f"pos_t{r}")
-            nc.sync.dma_start(pt[:], pos)
-            pos_t.append(pt)
 
-        all_bytes = keep.tile([P, T + WINDOW], U8, name="all_bytes", align_bytes=64)
+        all_bytes = keep.tile([P, T + 2 * WINDOW], U8, name="all_bytes", align_bytes=64)
         all_words = keep.tile([P, T + WINDOW], I32, name="all_words", align_bytes=64)
         nc.vector.memset(all_bytes[:, 2 * T :].bitcast(I32), 0)
         nc.vector.memset(all_words[:, 2 * T :], 0)
-        x_bytes = [all_bytes[:, T:], all_bytes[:, :WINDOW]]
+        x_bytes = [all_bytes[:, T:], all_bytes[:, : 2 * WINDOW]]
         x_words = [all_words[:, T:], all_words[:, :WINDOW]]
 
         def quantise_tokens(s, cut):
-            xb = keep.tile([P, T, 4], BF16, name=f"xb{s}", align_bytes=64)
-            for a, b in ((0, C), (C, cut)) if cut else ():
-                nc.vector.tensor_copy(
-                    out=xb[:, a:b, :].rearrange("p (c i) j -> p c j i", i=4),
-                    in_=raw[s][:, :, a:b].rearrange("p j (c i) -> p c j i", i=4),
+            xb = shared.tile([P, T, 4], BF16, name=f"xb{s}", align_bytes=64, offset=(1 - s) * 8192)
+            for u, (js, r) in enumerate(raw[s]):
+                for a, b in (((0, cut),), ((0, C), (C, cut)))[u] if cut else ():
+                    nc.vector.tensor_copy(
+                        out=xb[:, a:b, js].rearrange("p (c i) j -> p c j i", i=4),
+                        in_=r[:, :, a:b].rearrange("p j (c i) -> p c j i", i=4),
+                    )
+                nc.scalar.activation(
+                    xb[:, cut:, js].rearrange("p (c i) j -> p c j i", i=4),
+                    r[:, :, cut:].rearrange("p j (c i) -> p c j i", i=4),
+                    COPY,
                 )
-            nc.scalar.activation(
-                xb[:, cut:, :].rearrange("p (c i) j -> p c j i", i=4),
-                raw[s][:, :, cut:].rearrange("p j (c i) -> p c j i", i=4),
-                COPY,
-            )
             for cols in (slice(0, C), slice(C, T)):
                 nc.vector.quantize_mx(
                     out=x_words[s][:, cols].bitcast(FP8X4),
@@ -206,37 +208,59 @@ def tile_moe_tk_mlp_relu_kernel(
         on_vector = nc.vector.tensor_copy
         quantise_tokens(0, 288)
         early_bytes = bytes_tile(EARLY, "early_bytes")
-        early_words = words_tile(EARLY, "early_words")
-        for a, b in ((0, 2), (2, EARLY)):
-            gather_bytes(0, a, b, early_bytes[:, C * a : C * b])
-            gather_words(0, a, b, early_words[:, C * a : C * b])
+        early_words = words_tile(4, "early_words")
+        gather_words(0, 0, 2, early_words[:, : C * 2])
+        gather_bytes(0, 0, EARLY, early_bytes[:])
+        gather_words(0, 2, 4, early_words[:, C * 2 :])
         quantise_tokens(1, 0)
-        late_bytes = bytes_tile(E - EARLY, "raw1")
-        late_words = words_tile(E - EARLY, "xb1")
+        late_bytes = shared.tile([P, (E - EARLY) * C], U8, name="late_bytes", align_bytes=64, offset=0)
+        late_words = shared.tile([P, (E - 4) * C], U32, name="late_words", align_bytes=64, offset=1024)
         second_bytes = bytes_tile(E, "second_bytes")
         second_words = words_tile(E, "second_words")
         quads = [hidden_tile(0, 4), hidden_tile(4, 8)]
 
-        def first_pass(a, b):
+        def late_first_bytes(a, b):
             gather_bytes(0, a, b, late_bytes[:, C * (a - EARLY) : C * (b - EARLY)])
-            gather_words(0, a, b, late_words[:, C * (a - EARLY) : C * (b - EARLY)])
 
-        def second_pass(a, b):
+        def late_first_words(a, b):
+            gather_words(0, a, b, late_words[:, C * (a - 4) : C * (b - 4)])
+
+        def second_pass_bytes(a, b):
             gather_bytes(1, a, b, second_bytes[:, C * a : C * b])
+
+        def second_pass_words(a, b):
             gather_words(1, a, b, second_words[:, C * a : C * b])
 
-        second_pass(0, 2)
-        second_pass(2, EARLY)
-        for a, b in ((EARLY, 8), (8, 10)):
-            first_pass(a, b)
-            second_pass(a, b)
-        first_pass(10, E)
-        gather_bytes(1, 10, E, second_bytes[:, C * 10 :])
-        for e in (10, 11):
-            gather_words(1, e, e + 1, second_words[:, C * e : C * (e + 1)])
+        second_pass_bytes(0, 2)
+        second_pass_words(0, 2)
+        second_pass_bytes(2, 6)
+        second_pass_words(2, 4)
+        late_first_words(4, 6)
+        second_pass_words(4, 6)
+        late_first_bytes(6, 10)
+        for a in (6, 8):
+            late_first_words(a, a + 2)
+            second_pass_bytes(a, a + 2)
+            second_pass_words(a, a + 2)
+        late_first_bytes(10, E)
+        late_first_words(10, E)
+        second_pass_bytes(10, E)
+        second_pass_words(10, 11)
+        second_pass_words(11, E)
         for a in range(0, E, 2):
             first_product(a)
             first_product(a + 1)
+            if a == 0:
+                load_w1_scales(8, E, first_words[:].rearrange("p e s (h i) -> p (e s) h i", h=2))
+                load_w1(8)
+                load_w1(10)
+                load_w2(0, 8)
+                load_w2(8, E)
+                pos_t = []
+                for r, pos in enumerate((pos1, pos2, pos3, pos4)):
+                    pt = keep.tile([P, T // 16], U16, name=f"pos_t{r}")
+                    nc.sync.dma_start(pt[:], pos)
+                    pos_t.append(pt)
             if 2 <= a <= 8:
                 first = (a - 2) % 4
                 turn(a - 2, a, 4 + a // 2 % 2, quads[(a - 2) // 4][:, H * first : H * (first + 2)])

@@ -18,9 +18,15 @@ COPY = mybir.ActivationFunctionType.Copy
 K, T, E, C, H, N, TOP = 1024, 384, 12, 128, 512, 256, 4
 P = 128
 PASSES = K // 512
-WINDOW = 512
-EARLY = 6
-ROWS = (2, 4)
+WORD_WINDOW = 512
+BYTE_WINDOW = 1024
+ROWS_A_LOAD = (2, 4)
+VECTOR_TOKENS = (288, 0)
+EARLY_BYTES = 6
+EARLY_WORDS = 4
+ROUNDED_AT = (8192, 0)
+LATE_BYTES_AT = 0
+LATE_WORDS_AT = 1024
 FLOPS = 2 * TOP * T * (K * H + H * N)
 
 
@@ -36,25 +42,29 @@ def tile_moe_tk_mlp_relu_kernel(
         def bank(n, shape):
             return psum.tile(shape, F32, name=f"bank{n}")
 
+        on_scalar = nc.scalar.copy
+        on_vector = nc.vector.tensor_copy
+
         w1_words32 = w1_words.bitcast(I32)
         w1_scales32 = w1_scales.bitcast(I32)
         w2_words32 = w2_words.bitcast(I32)
         w2_scales32 = w2_scales.bitcast(I32)
-        raw = []
+        x_parts = []
         w1_at = {}
-        w1s_at = {}
+        w1_plane_at = {}
         w2_at = {}
 
         def load_x(s):
-            rows = xT[512 * s : 512 * (s + 1), :].rearrange("(p j) w -> p j w", j=4)
+            rows = xT[512 * s : 512 * (s + 1), :].rearrange("(p d) t -> p d t", d=4)
+            count = ROWS_A_LOAD[s]
             parts = []
-            for j in range(0, 4, ROWS[s]):
-                r = keep.tile([P, ROWS[s], T], F32, name=f"raw{s}{j}", align_bytes=64)
-                nc.sync.dma_start(out=r[:], in_=rows[:, j : j + ROWS[s], :])
-                parts.append((slice(j, j + ROWS[s]), r))
-            raw.append(parts)
+            for d in range(0, 4, count):
+                part = keep.tile([P, count, T], F32, name=f"raw{s}{d}", align_bytes=64)
+                nc.sync.dma_start(out=part[:], in_=rows[:, d : d + count, :])
+                parts.append((slice(d, d + count), part))
+            x_parts.append(parts)
 
-        def load_w1(a):
+        def load_w1_pair(a):
             w = keep.tile([P, 2, PASSES, 2 * H], U8, name=f"w1w{a}", align_bytes=64)
             nc.sync.dma_start(
                 out=w[:].rearrange("p e s w -> p (e s) w").bitcast(I32),
@@ -64,18 +74,19 @@ def tile_moe_tk_mlp_relu_kernel(
                 w1_at[a + e] = w[:, e]
             return w
 
-        def load_w1_scales(a, b, sc=None):
-            if sc is None:
-                sc = keep.tile([P, b - a, PASSES, H], U8, name=f"w1s{a}", align_bytes=64)
-                nc.vector.memset(sc[:].rearrange("p e s i -> p (e s i)").bitcast(I32), 0)
+        def zeroed_plane(a, b):
+            plane = keep.tile([P, b - a, PASSES, H], U8, name=f"w1s{a}", align_bytes=64)
+            nc.vector.memset(plane[:].rearrange("p e s i -> p (e s i)").bitcast(I32), 0)
+            return plane
+
+        def load_w1_scales(a, b, plane):
             for r in range(4):
                 nc.sync.dma_start(
-                    out=sc[r:P:32].rearrange("p e s i -> p (e s) i").bitcast(I32),
+                    out=plane[r:P:32].rearrange("p e s i -> p (e s) i").bitcast(I32),
                     in_=w1_scales32[a:b, :, r:16:4, :].rearrange("e s q i -> q (e s) i"),
                 )
             for e in range(a, b):
-                w1s_at[e] = sc[:, e - a]
-            return sc
+                w1_plane_at[e] = plane[:, e - a]
 
         def load_w2(a, b):
             w = keep.tile([P, b - a, 2 * N], U8, name=f"w2w{a}", align_bytes=64)
@@ -90,61 +101,60 @@ def tile_moe_tk_mlp_relu_kernel(
         offs_t = keep.tile([P, TOP * T // 16], U16, name="offs_t")
         nc.sync.dma_start(offs_t[:], offs)
         load_x(1)
-        first_words = load_w1(0)
-        load_w1(2)
-        first_plane = load_w1_scales(0, 4)
-        load_w1_scales(4, 8)
-        for a in range(4, 8, 2):
-            load_w1(a)
+        first_words = load_w1_pair(0)
+        load_w1_pair(2)
+        first_plane = zeroed_plane(0, 4)
+        load_w1_scales(0, 4, first_plane)
+        load_w1_scales(4, 8, zeroed_plane(4, 8))
+        load_w1_pair(4)
+        load_w1_pair(6)
 
-        all_bytes = keep.tile([P, T + 2 * WINDOW], U8, name="all_bytes", align_bytes=64)
-        all_words = keep.tile([P, T + WINDOW], I32, name="all_words", align_bytes=64)
+        all_bytes = keep.tile([P, T + BYTE_WINDOW], U8, name="all_bytes", align_bytes=64)
+        all_words = keep.tile([P, T + WORD_WINDOW], I32, name="all_words", align_bytes=64)
         nc.vector.memset(all_bytes[:, 2 * T :].bitcast(I32), 0)
         nc.vector.memset(all_words[:, 2 * T :], 0)
-        x_bytes = [all_bytes[:, T:], all_bytes[:, : 2 * WINDOW]]
-        x_words = [all_words[:, T:], all_words[:, :WINDOW]]
+        byte_window = [all_bytes[:, T:], all_bytes[:, :BYTE_WINDOW]]
+        word_window = [all_words[:, T:], all_words[:, :WORD_WINDOW]]
 
-        def quantise_tokens(s, cut):
-            xb = shared.tile([P, T, 4], BF16, name=f"xb{s}", align_bytes=64, offset=(1 - s) * 8192)
-            for u, (js, r) in enumerate(raw[s]):
-                for a, b in (((0, cut),), ((0, C), (C, cut)))[u] if cut else ():
+        def quantise_tokens(s):
+            rounded = shared.tile([P, T, 4], BF16, name=f"xb{s}", align_bytes=64, offset=ROUNDED_AT[s])
+            cut = VECTOR_TOKENS[s]
+            vector_shares = [[(0, cut)], [(0, C), (C, cut)]] if cut else [[]]
+            for shares, (rows, part) in zip(vector_shares, x_parts[s]):
+                for a, b in shares:
                     nc.vector.tensor_copy(
-                        out=xb[:, a:b, js].rearrange("p (c i) j -> p c j i", i=4),
-                        in_=r[:, :, a:b].rearrange("p j (c i) -> p c j i", i=4),
+                        out=rounded[:, a:b, rows].rearrange("p (c i) d -> p c d i", i=4),
+                        in_=part[:, :, a:b].rearrange("p d (c i) -> p c d i", i=4),
                     )
                 nc.scalar.activation(
-                    xb[:, cut:, js].rearrange("p (c i) j -> p c j i", i=4),
-                    r[:, :, cut:].rearrange("p j (c i) -> p c j i", i=4),
+                    rounded[:, cut:, rows].rearrange("p (c i) d -> p c d i", i=4),
+                    part[:, :, cut:].rearrange("p d (c i) -> p c d i", i=4),
                     COPY,
                 )
             for cols in (slice(0, C), slice(C, T)):
                 nc.vector.quantize_mx(
-                    out=x_words[s][:, cols].bitcast(FP8X4),
-                    scales=x_bytes[s][:, cols],
-                    in_=xb[:, cols, :].rearrange("p w j -> p (w j)"),
+                    out=word_window[s][:, cols].bitcast(FP8X4),
+                    scales=byte_window[s][:, cols],
+                    in_=rounded[:, cols, :].rearrange("p t d -> p (t d)"),
                 )
 
-        y_t = [keep.tile([P, TOP * T], F32, name=f"y_t{h}") for h in range(2)]
+        y_t = [keep.tile([P, TOP * T], F32, name=f"y_t{half}") for half in range(2)]
         bytes_at = {}
         words_at = {}
         act_at = {}
         hidden_at = {}
 
-        def gather_bytes(s, a, b, gb):
-            nc.vector.tensor_copy(gb, x_bytes[s].indirect(offs_t[:, C // 16 * a : C // 16 * b]))
+        def gather_bytes(s, a, b, tile, first):
+            slots = tile[:, C * (a - first) : C * (b - first)]
+            nc.vector.tensor_copy(slots, byte_window[s].indirect(offs_t[:, C // 16 * a : C // 16 * b]))
             for e in range(a, b):
-                bytes_at[e, s] = gb[:, C * (e - a) : C * (e - a + 1)]
+                bytes_at[e, s] = slots[:, C * (e - a) : C * (e - a + 1)]
 
-        def bytes_tile(n, name):
-            return keep.tile([P, n * C], U8, name=name, align_bytes=64)
-
-        def gather_words(s, a, b, gw):
-            nc.vector.tensor_copy(gw, x_words[s].bitcast(U32).indirect(offs_t[:, C // 16 * a : C // 16 * b]))
+        def gather_words(s, a, b, tile, first):
+            slots = tile[:, C * (a - first) : C * (b - first)]
+            nc.vector.tensor_copy(slots, word_window[s].bitcast(U32).indirect(offs_t[:, C // 16 * a : C // 16 * b]))
             for e in range(a, b):
-                words_at[e, s] = gw[:, C * (e - a) : C * (e - a + 1)]
-
-        def words_tile(n, name):
-            return keep.tile([P, n * C], U32, name=name, align_bytes=64)
+                words_at[e, s] = slots[:, C * (e - a) : C * (e - a + 1)]
 
         def first_product(e):
             acc = bank(e % 4, [P, H])
@@ -154,19 +164,19 @@ def tile_moe_tk_mlp_relu_kernel(
                     lhsT=words_at[e, s].bitcast(FP8X4),
                     lhsT_scale=bytes_at[e, s],
                     rhs=w1_at[e][:, s, :].bitcast(FP4X4),
-                    rhs_scale=w1s_at[e][:, s, :],
+                    rhs_scale=w1_plane_at[e][:, s, :],
                     start=(s == 0),
                     stop=(s == PASSES - 1),
                 )
-            act = keep.tile([P, H], BF16, name=f"act{e}")
+            act = keep.tile([P, H], BF16, name=f"act{e}", align_bytes=64)
             nc.scalar.activation(
-                act[:].rearrange("p (u m d) -> p u m d", u=2, d=2),
-                acc[:].rearrange("p (m u d) -> p u m d", u=2, d=2),
+                act[:].rearrange("p (u m j) -> p u m j", u=2, j=2),
+                acc[:].rearrange("p (m u j) -> p u m j", u=2, j=2),
                 RELU,
             )
             act_at[e] = act
 
-        def turn(a, b, n, ht, copy=nc.scalar.copy):
+        def turn(a, b, n, hidden, copy):
             turned = bank(n, [P, b - a, 2, C])
             for e in range(a, b):
                 for u in range(2):
@@ -174,156 +184,165 @@ def tile_moe_tk_mlp_relu_kernel(
                         turned[:, e - a, u, :], act_at[e][:].bitcast(F32)[:, C * u : C * (u + 1)], ident[:]
                     )
             copy(
-                out=ht.bitcast(F32).rearrange("p (i r u) -> p i r u", i=b - a, u=2),
-                in_=turned[:].rearrange("p i u r -> p i r u"),
+                out=hidden.bitcast(F32).rearrange("p (e c u) -> p e c u", e=b - a, u=2),
+                in_=turned[:].rearrange("p e u c -> p e c u"),
             )
 
         def hidden_tile(a, b):
             return keep.tile([P, (b - a) * H], BF16, name=f"ht{a}", align_bytes=64)
 
-        def quantise_hidden(a, b, ht):
-            hw = keep.tile([P, (b - a) * C], U32, name=f"hw{a}", align_bytes=64)
-            hb = keep.tile([P, (b - a) * C], U8, name=f"hb{a}", align_bytes=64)
-            nc.vector.quantize_mx(out=hw[:].bitcast(FP8X4), scales=hb[:], in_=ht[:])
+        def quantise_hidden(a, b, hidden, plane_tag):
+            words = keep.tile([P, (b - a) * C], U32, name=f"hw{a}", align_bytes=64)
+            plane = keep.tile([P, (b - a) * C], U8, name=plane_tag, align_bytes=64)
+            nc.vector.quantize_mx(out=words[:].bitcast(FP8X4), scales=plane[:], in_=hidden[:])
             for e in range(a, b):
                 cols = slice(C * (e - a), C * (e - a + 1))
-                hidden_at[e] = (hw[:, cols], hb[:, cols])
+                hidden_at[e] = (words[:, cols], plane[:, cols])
 
-        def second_product(h, a, b, n, copy=nc.scalar.copy):
-            yp = bank(n, [P, (b - a) * C])
+        def second_product(half, a, b, n, copy):
+            sums = bank(n, [P, (b - a) * C])
             for e in range(a, b):
-                hw, hb = hidden_at[e]
+                words, plane = hidden_at[e]
                 nc.tensor.matmul_mx(
-                    out=yp[:, C * (e - a) : C * (e - a + 1)],
-                    lhsT=w2_at[e][:, 2 * P * h : 2 * P * (h + 1)].bitcast(FP4X4),
-                    lhsT_scale=w2s[:, e, P * h : P * (h + 1)],
-                    rhs=hw.bitcast(FP8X4),
-                    rhs_scale=hb,
+                    out=sums[:, C * (e - a) : C * (e - a + 1)],
+                    lhsT=w2_at[e][:, 2 * P * half : 2 * P * (half + 1)].bitcast(FP4X4),
+                    lhsT_scale=w2_plane[:, e, P * half : P * (half + 1)],
+                    rhs=words.bitcast(FP8X4),
+                    rhs_scale=plane,
                     start=True,
                     stop=True,
                 )
-            copy(out=y_t[h][:, C * a : C * b], in_=yp[:])
+            copy(out=y_t[half][:, C * a : C * b], in_=sums[:])
 
-        on_scalar = nc.scalar.copy
-        on_vector = nc.vector.tensor_copy
-        quantise_tokens(0, 288)
-        early_bytes = bytes_tile(EARLY, "early_bytes")
-        early_words = words_tile(4, "early_words")
-        gather_words(0, 0, 2, early_words[:, : C * 2])
-        gather_bytes(0, 0, EARLY, early_bytes[:])
-        gather_words(0, 2, 4, early_words[:, C * 2 :])
-        quantise_tokens(1, 0)
-        late_bytes = shared.tile([P, (E - EARLY) * C], U8, name="late_bytes", align_bytes=64, offset=0)
-        late_words = shared.tile([P, (E - 4) * C], U32, name="late_words", align_bytes=64, offset=1024)
-        second_bytes = bytes_tile(E, "second_bytes")
-        second_words = words_tile(E, "second_words")
+        quantise_tokens(0)
+        early_bytes = keep.tile([P, EARLY_BYTES * C], U8, name="early_bytes", align_bytes=64)
+        early_words = keep.tile([P, EARLY_WORDS * C], U32, name="early_words", align_bytes=64)
+        gather_words(0, 0, 2, early_words, 0)
+        gather_bytes(0, 0, EARLY_BYTES, early_bytes, 0)
+        gather_words(0, 2, EARLY_WORDS, early_words, 0)
+        quantise_tokens(1)
+        late_bytes = shared.tile(
+            [P, (E - EARLY_BYTES) * C], U8, name="late_bytes", align_bytes=64, offset=LATE_BYTES_AT
+        )
+        late_words = shared.tile(
+            [P, (E - EARLY_WORDS) * C], U32, name="late_words", align_bytes=64, offset=LATE_WORDS_AT
+        )
+        second_bytes = keep.tile([P, E * C], U8, name="second_bytes", align_bytes=64)
+        second_words = keep.tile([P, E * C], U32, name="second_words", align_bytes=64)
         quads = [hidden_tile(0, 4), hidden_tile(4, 8)]
 
-        def late_first_bytes(a, b):
-            gather_bytes(0, a, b, late_bytes[:, C * (a - EARLY) : C * (b - EARLY)])
+        def first_pass_bytes(a, b):
+            gather_bytes(0, a, b, late_bytes, EARLY_BYTES)
 
-        def late_first_words(a, b):
-            gather_words(0, a, b, late_words[:, C * (a - 4) : C * (b - 4)])
+        def first_pass_words(a, b):
+            gather_words(0, a, b, late_words, EARLY_WORDS)
 
         def second_pass_bytes(a, b):
-            gather_bytes(1, a, b, second_bytes[:, C * a : C * b])
+            gather_bytes(1, a, b, second_bytes, 0)
 
         def second_pass_words(a, b):
-            gather_words(1, a, b, second_words[:, C * a : C * b])
+            gather_words(1, a, b, second_words, 0)
 
         second_pass_bytes(0, 2)
         second_pass_words(0, 2)
-        second_pass_bytes(2, 6)
+        second_pass_bytes(2, 8)
         second_pass_words(2, 4)
-        late_first_words(4, 6)
+        first_pass_words(4, 7)
         second_pass_words(4, 6)
-        late_first_bytes(6, 10)
-        for a in (6, 8):
-            late_first_words(a, a + 2)
-            second_pass_bytes(a, a + 2)
-            second_pass_words(a, a + 2)
-        late_first_bytes(10, E)
-        late_first_words(10, E)
+        first_pass_bytes(6, 10)
+        second_pass_words(6, 7)
+        first_pass_words(7, 10)
+        second_pass_words(7, 8)
+        second_pass_bytes(8, 10)
+        second_pass_words(8, 10)
+        first_pass_bytes(10, E)
         second_pass_bytes(10, E)
-        second_pass_words(10, 11)
-        second_pass_words(11, E)
+        for e in (10, 11):
+            first_pass_words(e, e + 1)
+            second_pass_words(e, e + 1)
+
+        pos_t = []
         for a in range(0, E, 2):
             first_product(a)
             first_product(a + 1)
             if a == 0:
-                load_w1_scales(8, E, first_words[:].rearrange("p e s (h i) -> p (e s) h i", h=2))
-                load_w1(8)
-                load_w1(10)
+                load_w1_scales(8, E, first_words[:].rearrange("p e s (g i) -> p (e s) g i", g=PASSES))
+                load_w1_pair(8)
+                load_w1_pair(10)
                 load_w2(0, 8)
                 load_w2(8, E)
-                pos_t = []
                 for r, pos in enumerate((pos1, pos2, pos3, pos4)):
-                    pt = keep.tile([P, T // 16], U16, name=f"pos_t{r}")
-                    nc.sync.dma_start(pt[:], pos)
-                    pos_t.append(pt)
+                    listed = keep.tile([P, T // 16], U16, name=f"pos_t{r}")
+                    nc.sync.dma_start(listed[:], pos)
+                    pos_t.append(listed)
             if 2 <= a <= 8:
-                first = (a - 2) % 4
-                turn(a - 2, a, 4 + a // 2 % 2, quads[(a - 2) // 4][:, H * first : H * (first + 2)])
-        w2s = first_plane[:].rearrange("p e s i -> p (e s i)")[:, : E * N].rearrange("p (e n) -> p e n", n=N)
+                place = (a - 2) % 4
+                turn(a - 2, a, 4 + a // 2 % 2, quads[(a - 2) // 4][:, H * place : H * (place + 2)], on_scalar)
+
+        w2_plane = first_plane[:].rearrange("p e s i -> p (e s i)")[:, : E * N].rearrange("p (e n) -> p e n", n=N)
         for r in range(4):
             nc.sync.dma_start(
-                out=w2s[r:P:32].bitcast(I32),
+                out=w2_plane[r:P:32].bitcast(I32),
                 in_=w2_scales32[:, 0, r:16:4, :].rearrange("e q n -> q e n"),
             )
         gate_t = keep.tile([P, TOP, T], F32, name="gate_t", align_bytes=64)
         nc.sync.dma_start(out=gate_t[:], in_=gate[:, 0:P, :].rearrange("r p t -> p r t"))
-        quantise_hidden(0, 4, quads[0])
-        quantise_hidden(4, 8, quads[1])
-        for a, b, n, copy in ((8, 10, 0, on_vector), (10, 11, 4, on_scalar), (11, 12, 5, on_scalar)):
-            ht = hidden_tile(a, b)
-            turn(a, b, n, ht[:], copy)
-            quantise_hidden(a, b, ht)
-        second_product(0, 0, 4, 6)
-        second_product(0, 4, 8, 7, on_vector)
-        second_product(0, 8, 10, 1)
-        second_product(0, 10, 12, 3)
-        second_product(1, 8, 12, 5)
-        second_product(1, 0, 4, 1)
-        second_product(1, 4, 8, 5)
 
-        def fetch(h, r, z, cols):
+        quantise_hidden(0, 4, quads[0], "hb0")
+        quantise_hidden(4, 8, quads[1], "hb4")
+        pair, tenth, eleventh = hidden_tile(8, 10), hidden_tile(10, 11), hidden_tile(11, E)
+        turn(8, 10, 0, pair[:], on_vector)
+        turn(10, 11, 4, tenth[:], on_scalar)
+        turn(11, E, 5, eleventh[:], on_scalar)
+        quantise_hidden(10, 11, tenth, "hb10")
+        quantise_hidden(8, 10, pair, "act11")
+        quantise_hidden(11, E, eleventh, "hb11")
+        second_product(0, 0, 4, 6, on_scalar)
+        second_product(0, 4, 8, 7, on_vector)
+        second_product(0, 8, 10, 1, on_scalar)
+        second_product(0, 10, E, 3, on_scalar)
+        second_product(1, 8, E, 5, on_scalar)
+        second_product(1, 0, 4, 1, on_scalar)
+        second_product(1, 4, 8, 5, on_scalar)
+
+        def fetch(half, r, term, cols):
             nc.vector.tensor_tensor(
-                z[:, cols],
-                y_t[h][:].indirect(pos_t[r][:, cols.start // 16 : cols.stop // 16]),
+                term[:, cols],
+                y_t[half][:].indirect(pos_t[r][:, cols.start // 16 : cols.stop // 16]),
                 gate_t[:, r, cols],
                 MULT,
             )
 
-        blocks = [slice(C * b, C * (b + 1)) for b in range(3)]
+        blocks = [slice(C * b, C * (b + 1)) for b in range(T // C)]
 
-        def summed_on_tensor(h, terms, back):
+        def summed_on_tensor(half, terms, last_term_cols, back):
             acc = [bank(n, [P, C]) for n in (0, 2, 6)]
             for r in range(terms):
-                z = keep.tile([P, T], F32, name=f"z{h}{r}")
-                for cols in blocks if (h, r) == (1, terms - 1) else [slice(0, T)]:
-                    fetch(h, r, z, cols)
-                for b in range(3):
+                term = keep.tile([P, T], F32, name=f"z{half}{r}")
+                for cols in last_term_cols if r == terms - 1 else [slice(0, T)]:
+                    fetch(half, r, term, cols)
+                for b, cols in enumerate(blocks):
                     nc.tensor.matmul(
                         acc[b][:],
-                        lhsT=z[:, blocks[b]],
+                        lhsT=term[:, cols],
                         rhs=ident[:],
                         is_transpose=True,
                         start=(r == 0),
                         stop=(r == terms - 1),
                     )
-            summed = keep.tile([P, 3, C], F32, name=f"summed{h}")
-            for b in range(3):
+            summed = keep.tile([P, len(blocks), C], F32, name=f"summed{half}")
+            for b in range(len(blocks)):
                 nc.scalar.copy(out=summed[:, b, :], in_=acc[b][:])
                 nc.tensor.transpose(back[b], summed[:, b, :], ident[:])
 
-        total = [keep.tile([P, T], F32, name=f"total{h}") for h in range(2)]
+        total = [keep.tile([P, T], F32, name=f"total{half}") for half in range(2)]
         back = bank(4, [P, T])
-        summed_on_tensor(0, TOP, [back[:, cols] for cols in blocks])
+        summed_on_tensor(0, TOP, [slice(0, T)], [back[:, cols] for cols in blocks])
         nc.scalar.copy(out=total[0][:], in_=back[:])
         nc.sync.dma_start(out=out[0:P, :], in_=total[0][:])
         pieces = (slice(0, 2 * C), slice(2 * C, T))
         backs = [bank(7, [P, 2 * C]), bank(3, [P, C])]
-        summed_on_tensor(1, TOP - 1, [backs[0][:, :C], backs[0][:, C:], backs[1][:]])
+        summed_on_tensor(1, TOP - 1, blocks, [backs[0][:, :C], backs[0][:, C:], backs[1][:]])
         last = keep.tile([P, T], F32, name="last")
         for cols in pieces:
             fetch(1, TOP - 1, last, cols)

@@ -20,8 +20,8 @@ P = 128
 PASSES = K // 512
 WORD_WINDOW = 512
 BYTE_WINDOW = 1024
-ROWS_A_LOAD = (2, 4)
-VECTOR_TOKENS = (288, 0)
+PIECES = (slice(0, 2 * C), slice(2 * C, T))
+VECTOR_TOKENS = ((184, 96), (0, 0))
 EARLY_BYTES = 6
 EARLY_WORDS = 4
 ROUNDED_AT = (8192, 0)
@@ -56,12 +56,11 @@ def tile_moe_tk_mlp_relu_kernel(
 
         def load_x(s):
             rows = xT[512 * s : 512 * (s + 1), :].rearrange("(p d) t -> p d t", d=4)
-            count = ROWS_A_LOAD[s]
             parts = []
-            for d in range(0, 4, count):
-                part = keep.tile([P, count, T], F32, name=f"raw{s}{d}", align_bytes=64)
-                nc.sync.dma_start(out=part[:], in_=rows[:, d : d + count, :])
-                parts.append((slice(d, d + count), part))
+            for cols in PIECES:
+                part = keep.tile([P, 4, cols.stop - cols.start], F32, name=f"raw{s}_{cols.start}", align_bytes=64)
+                nc.sync.dma_start(out=part[:], in_=rows[:, :, cols])
+                parts.append(part)
             x_parts.append(parts)
 
         def load_w1_pair(a):
@@ -118,20 +117,19 @@ def tile_moe_tk_mlp_relu_kernel(
 
         def quantise_tokens(s):
             rounded = shared.tile([P, T, 4], BF16, name=f"xb{s}", align_bytes=64, offset=ROUNDED_AT[s])
-            cut = VECTOR_TOKENS[s]
-            vector_shares = [[(0, cut)], [(0, C), (C, cut)]] if cut else [[]]
-            for shares, (rows, part) in zip(vector_shares, x_parts[s]):
-                for a, b in shares:
+            for cols, cut, part in zip(PIECES, VECTOR_TOKENS[s], x_parts[s]):
+                piece = rounded[:, cols, :]
+                if cut:
                     nc.vector.tensor_copy(
-                        out=rounded[:, a:b, rows].rearrange("p (c i) d -> p c d i", i=4),
-                        in_=part[:, :, a:b].rearrange("p d (c i) -> p c d i", i=4),
+                        out=piece[:, :cut, :].rearrange("p (c i) d -> p c d i", i=4),
+                        in_=part[:, :, :cut].rearrange("p d (c i) -> p c d i", i=4),
                     )
                 nc.scalar.activation(
-                    rounded[:, cut:, rows].rearrange("p (c i) d -> p c d i", i=4),
+                    piece[:, cut:, :].rearrange("p (c i) d -> p c d i", i=4),
                     part[:, :, cut:].rearrange("p d (c i) -> p c d i", i=4),
                     COPY,
                 )
-            for cols in (slice(0, C), slice(C, T)):
+            for cols in PIECES:
                 nc.vector.quantize_mx(
                     out=word_window[s][:, cols].bitcast(FP8X4),
                     scales=byte_window[s][:, cols],
@@ -289,63 +287,83 @@ def tile_moe_tk_mlp_relu_kernel(
         nc.sync.dma_start(out=gate_t[:], in_=gate[:, 0:P, :].rearrange("r p t -> p r t"))
 
         quantise_hidden(0, 4, quads[0], "hb0")
-        quantise_hidden(4, 8, quads[1], "hb4")
         pair, tenth, eleventh = hidden_tile(8, 10), hidden_tile(10, 11), hidden_tile(11, E)
         turn(8, 10, 0, pair[:], on_vector)
+        quantise_hidden(4, 8, quads[1], "hb4")
         turn(10, 11, 4, tenth[:], on_scalar)
         turn(11, E, 5, eleventh[:], on_scalar)
         quantise_hidden(10, 11, tenth, "hb10")
         quantise_hidden(8, 10, pair, "act11")
         quantise_hidden(11, E, eleventh, "hb11")
-        second_product(0, 0, 4, 6, on_scalar)
-        second_product(0, 4, 8, 7, on_vector)
-        second_product(0, 8, 10, 1, on_scalar)
-        second_product(0, 10, E, 3, on_scalar)
-        second_product(1, 8, E, 5, on_scalar)
-        second_product(1, 0, 4, 1, on_scalar)
-        second_product(1, 4, 8, 5, on_scalar)
+        second_product(1, 0, 4, 6, on_scalar)
+        second_product(0, 0, 4, 7, on_vector)
+        second_product(1, 4, 8, 1, on_scalar)
+        second_product(0, 4, 6, 2, on_vector)
+        second_product(0, 6, 8, 0, on_scalar)
+        second_product(0, 8, E, 3, on_vector)
+        second_product(1, 8, E, 4, on_scalar)
 
-        def fetch(half, r, term, cols):
-            nc.vector.tensor_tensor(
-                term[:, cols],
-                y_t[half][:].indirect(pos_t[r][:, cols.start // 16 : cols.stop // 16]),
-                gate_t[:, r, cols],
-                MULT,
-            )
-
+        whole = slice(0, T)
         blocks = [slice(C * b, C * (b + 1)) for b in range(T // C)]
 
-        def summed_on_tensor(half, terms, last_term_cols, back):
-            acc = [bank(n, [P, C]) for n in (0, 2, 6)]
-            for r in range(terms):
-                term = keep.tile([P, T], F32, name=f"z{half}{r}")
-                for cols in last_term_cols if r == terms - 1 else [slice(0, T)]:
-                    fetch(half, r, term, cols)
-                for b, cols in enumerate(blocks):
-                    nc.tensor.matmul(
-                        acc[b][:],
-                        lhsT=term[:, cols],
-                        rhs=ident[:],
-                        is_transpose=True,
-                        start=(r == 0),
-                        stop=(r == terms - 1),
-                    )
-            summed = keep.tile([P, len(blocks), C], F32, name=f"summed{half}")
+        def listed(r, cols):
+            return pos_t[r][:, cols.start // 16 : cols.stop // 16]
+
+        def fetch(half, r, term, cols):
+            nc.vector.tensor_tensor(term[:, cols], y_t[half][:].indirect(listed(r, cols)), gate_t[:, r, cols], MULT)
+
+        def fetch_plain(half, r):
+            plain = keep.tile([P, T], F32, name=f"plain{half}{r}")
+            nc.scalar.activation(plain[:], y_t[half][:].indirect(pos_t[r][:]), COPY)
+            return plain
+
+        def weigh(r, plain, term, cols):
+            nc.vector.tensor_tensor(term[:, cols], plain[:, cols], gate_t[:, r, cols], MULT)
+
+        def add_on_tensor(acc, term, first, last):
+            for b, cols in enumerate(blocks):
+                nc.tensor.matmul(acc[b][:], lhsT=term[:, cols], rhs=ident[:], is_transpose=True, start=first, stop=last)
+
+        def turn_back(tag, acc, back):
+            summed = keep.tile([P, len(blocks), C], F32, name=tag)
             for b in range(len(blocks)):
                 nc.scalar.copy(out=summed[:, b, :], in_=acc[b][:])
                 nc.tensor.transpose(back[b], summed[:, b, :], ident[:])
 
-        total = [keep.tile([P, T], F32, name=f"total{half}") for half in range(2)]
-        back = bank(4, [P, T])
-        summed_on_tensor(0, TOP, [slice(0, T)], [back[:, cols] for cols in blocks])
+        plain = {(half, r): fetch_plain(half, r) for half in range(2) for r in (2, 3)}
+
+        acc = [bank(n, [P, C]) for n in (5, 6, 7)]
+        for r in range(TOP):
+            term = keep.tile([P, T], F32, name=f"term0{r}")
+            if r < 2:
+                fetch(0, r, term, whole)
+            else:
+                weigh(r, plain[0, r], term, whole)
+            add_on_tensor(acc, term, r == 0, r == TOP - 1)
+        first_acc = acc
+
+        acc = [bank(n, [P, C]) for n in (0, 1, 2)]
+        term = keep.tile([P, T], F32, name="plain02")
+        fetch(1, 0, term, whole)
+        add_on_tensor(acc, term, True, False)
+        term = keep.tile([P, T], F32, name="term12")
+        weigh(2, plain[1, 2], term, whole)
+        add_on_tensor(acc, term, False, False)
+        term = keep.tile([P, T], F32, name="term13")
+        for cols in blocks:
+            weigh(3, plain[1, 3], term, cols)
+        add_on_tensor(acc, term, False, True)
+        back = bank(3, [P, T])
+        turn_back("summed0", first_acc, [back[:, cols] for cols in blocks])
+        pieces = (slice(0, 2 * C), slice(2 * C, T))
+        backs = [bank(4, [P, 2 * C]), bank(5, [P, C])]
+        turn_back("summed1", acc, [backs[0][:, :C], backs[0][:, C:], backs[1][:]])
+        total = [keep.tile([P, T], F32, name="term13"), keep.tile([P, T], F32, name="total1")]
         nc.scalar.copy(out=total[0][:], in_=back[:])
         nc.sync.dma_start(out=out[0:P, :], in_=total[0][:])
-        pieces = (slice(0, 2 * C), slice(2 * C, T))
-        backs = [bank(7, [P, 2 * C]), bank(3, [P, C])]
-        summed_on_tensor(1, TOP - 1, blocks, [backs[0][:, :C], backs[0][:, C:], backs[1][:]])
-        last = keep.tile([P, T], F32, name="last")
+        last = keep.tile([P, T], F32, name="plain12")
         for cols in pieces:
-            fetch(1, TOP - 1, last, cols)
+            fetch(1, 1, last, cols)
         for b, cols in enumerate(pieces):
             nc.vector.tensor_add(total[1][:, cols], last[:, cols], backs[b][:])
             nc.sync.dma_start(out=out[P:, cols], in_=total[1][:, cols])

@@ -20,8 +20,8 @@ P = 128
 PASSES = K // 512
 WORD_WINDOW = 512
 BYTE_WINDOW = 1024
-PIECES = (slice(0, 2 * C), slice(2 * C, T))
-VECTOR_TOKENS = ((184, 96), (0, 0))
+ROWS_A_LOAD = (2, 4)
+VECTOR_TOKENS = (288, 0)
 EARLY_BYTES = 6
 EARLY_WORDS = 4
 ROUNDED_AT = (8192, 0)
@@ -56,11 +56,12 @@ def tile_moe_tk_mlp_relu_kernel(
 
         def load_x(s):
             rows = xT[512 * s : 512 * (s + 1), :].rearrange("(p d) t -> p d t", d=4)
+            count = ROWS_A_LOAD[s]
             parts = []
-            for cols in PIECES:
-                part = keep.tile([P, 4, cols.stop - cols.start], F32, name=f"raw{s}_{cols.start}", align_bytes=64)
-                nc.sync.dma_start(out=part[:], in_=rows[:, :, cols])
-                parts.append(part)
+            for d in range(0, 4, count):
+                part = keep.tile([P, count, T], F32, name=f"raw{s}{d}", align_bytes=64)
+                nc.sync.dma_start(out=part[:], in_=rows[:, d : d + count, :])
+                parts.append((slice(d, d + count), part))
             x_parts.append(parts)
 
         def load_w1_pair(a):
@@ -117,19 +118,20 @@ def tile_moe_tk_mlp_relu_kernel(
 
         def quantise_tokens(s):
             rounded = shared.tile([P, T, 4], BF16, name=f"xb{s}", align_bytes=64, offset=ROUNDED_AT[s])
-            for cols, cut, part in zip(PIECES, VECTOR_TOKENS[s], x_parts[s]):
-                piece = rounded[:, cols, :]
-                if cut:
+            cut = VECTOR_TOKENS[s]
+            vector_shares = [[(0, cut)], [(0, C), (C, cut)]] if cut else [[]]
+            for shares, (rows, part) in zip(vector_shares, x_parts[s]):
+                for a, b in shares:
                     nc.vector.tensor_copy(
-                        out=piece[:, :cut, :].rearrange("p (c i) d -> p c d i", i=4),
-                        in_=part[:, :, :cut].rearrange("p d (c i) -> p c d i", i=4),
+                        out=rounded[:, a:b, rows].rearrange("p (c i) d -> p c d i", i=4),
+                        in_=part[:, :, a:b].rearrange("p d (c i) -> p c d i", i=4),
                     )
                 nc.scalar.activation(
-                    piece[:, cut:, :].rearrange("p (c i) d -> p c d i", i=4),
+                    rounded[:, cut:, rows].rearrange("p (c i) d -> p c d i", i=4),
                     part[:, :, cut:].rearrange("p d (c i) -> p c d i", i=4),
                     COPY,
                 )
-            for cols in PIECES:
+            for cols in (slice(0, C), slice(C, T)):
                 nc.vector.quantize_mx(
                     out=word_window[s][:, cols].bitcast(FP8X4),
                     scales=byte_window[s][:, cols],

@@ -21,12 +21,11 @@ PASSES = K // 512
 WORD_WINDOW = 512
 BYTE_WINDOW = 1024
 ROWS_A_LOAD = (2, 4)
-VECTOR_TOKENS = (288, 0)
+VECTOR_TOKENS = 288
 EARLY_BYTES = 6
 EARLY_WORDS = 4
-ROUNDED_AT = (8192, 0)
-LATE_BYTES_AT = 0
-LATE_WORDS_AT = 1024
+LATE_BYTES_AT = 2048
+LATE_WORDS_AT = 2816
 FLOPS = 2 * TOP * T * (K * H + H * N)
 
 
@@ -116,27 +115,41 @@ def tile_moe_tk_mlp_relu_kernel(
         byte_window = [all_bytes[:, T:], all_bytes[:, :BYTE_WINDOW]]
         word_window = [all_words[:, T:], all_words[:, :WORD_WINDOW]]
 
-        def quantise_tokens(s):
-            rounded = shared.tile([P, T, 4], BF16, name=f"xb{s}", align_bytes=64, offset=ROUNDED_AT[s])
-            cut = VECTOR_TOKENS[s]
-            vector_shares = [[(0, cut)], [(0, C), (C, cut)]] if cut else [[]]
-            for shares, (rows, part) in zip(vector_shares, x_parts[s]):
-                for a, b in shares:
+        def by_fours(view, order):
+            return view.rearrange(order + " -> p c d i", i=4)
+
+        def quantise_tokens(s, cols, rounded):
+            nc.vector.quantize_mx(
+                out=word_window[s][:, cols].bitcast(FP8X4),
+                scales=byte_window[s][:, cols],
+                in_=rounded.rearrange("p t d -> p (t d)"),
+            )
+
+        def first_pass_tokens():
+            rounded = keep.tile([P, T, 4], BF16, name="rounded", align_bytes=64)
+            shares = [[(0, VECTOR_TOKENS)], [(0, C), (C, VECTOR_TOKENS)]]
+            for share, (rows, part) in zip(shares, x_parts[0]):
+                for a, b in share:
                     nc.vector.tensor_copy(
-                        out=rounded[:, a:b, rows].rearrange("p (c i) d -> p c d i", i=4),
-                        in_=part[:, :, a:b].rearrange("p d (c i) -> p c d i", i=4),
+                        out=by_fours(rounded[:, a:b, rows], "p (c i) d"), in_=by_fours(part[:, :, a:b], "p d (c i)")
                     )
                 nc.scalar.activation(
-                    rounded[:, cut:, rows].rearrange("p (c i) d -> p c d i", i=4),
-                    part[:, :, cut:].rearrange("p d (c i) -> p c d i", i=4),
+                    by_fours(rounded[:, VECTOR_TOKENS:, rows], "p (c i) d"),
+                    by_fours(part[:, :, VECTOR_TOKENS:], "p d (c i)"),
                     COPY,
                 )
             for cols in (slice(0, C), slice(C, T)):
-                nc.vector.quantize_mx(
-                    out=word_window[s][:, cols].bitcast(FP8X4),
-                    scales=byte_window[s][:, cols],
-                    in_=rounded[:, cols, :].rearrange("p t d -> p (t d)"),
+                quantise_tokens(0, cols, rounded[:, cols, :])
+
+        def second_pass_tokens():
+            for cols in (slice(0, 2 * C), slice(2 * C, T)):
+                rounded = shared.tile(
+                    [P, cols.stop - cols.start, 4], BF16, name=f"rounded{cols.start}", align_bytes=64, offset=8 * cols.start
                 )
+                nc.scalar.activation(
+                    by_fours(rounded[:], "p (c i) d"), by_fours(x_parts[1][0][1][:, :, cols], "p d (c i)"), COPY
+                )
+                quantise_tokens(1, cols, rounded[:])
 
         y_t = [keep.tile([P, TOP * T], F32, name=f"y_t{half}") for half in range(2)]
         bytes_at = {}
@@ -214,13 +227,14 @@ def tile_moe_tk_mlp_relu_kernel(
                 )
             copy(out=y_t[half][:, C * a : C * b], in_=sums[:])
 
-        quantise_tokens(0)
+        first_pass_tokens()
         early_bytes = keep.tile([P, EARLY_BYTES * C], U8, name="early_bytes", align_bytes=64)
-        early_words = keep.tile([P, EARLY_WORDS * C], U32, name="early_words", align_bytes=64)
+        early_words = keep.tile([P, 2 * C], U32, name="early_words", align_bytes=64)
         gather_words(0, 0, 2, early_words, 0)
         gather_bytes(0, 0, EARLY_BYTES, early_bytes, 0)
-        gather_words(0, 2, EARLY_WORDS, early_words, 0)
-        quantise_tokens(1)
+        second_pass_tokens()
+        between = shared.tile([P, 2 * C], U32, name="between", align_bytes=64, offset=0)
+        gather_words(0, 2, EARLY_WORDS, between, 2)
         late_bytes = shared.tile(
             [P, (E - EARLY_BYTES) * C], U8, name="late_bytes", align_bytes=64, offset=LATE_BYTES_AT
         )
@@ -299,11 +313,12 @@ def tile_moe_tk_mlp_relu_kernel(
         quantise_hidden(11, E, eleventh, "hb11")
         second_product(1, 0, 4, 6, on_scalar)
         second_product(0, 0, 4, 7, on_vector)
+        second_product(0, 4, 8, 2, on_scalar)
         second_product(1, 4, 8, 1, on_scalar)
-        second_product(0, 4, 6, 2, on_vector)
-        second_product(0, 6, 8, 0, on_scalar)
-        second_product(0, 8, E, 3, on_vector)
-        second_product(1, 8, E, 4, on_scalar)
+        second_product(0, 8, 10, 0, on_vector)
+        second_product(0, 10, E, 3, on_vector)
+        second_product(1, 11, E, 5, on_vector)
+        second_product(1, 8, 11, 4, on_scalar)
 
         whole = slice(0, T)
         blocks = [slice(C * b, C * (b + 1)) for b in range(T // C)]
@@ -314,9 +329,10 @@ def tile_moe_tk_mlp_relu_kernel(
         def fetch(half, r, term, cols):
             nc.vector.tensor_tensor(term[:, cols], y_t[half][:].indirect(listed(r, cols)), gate_t[:, r, cols], MULT)
 
-        def fetch_plain(half, r):
+        def fetch_plain(half, r, pieces):
             plain = keep.tile([P, T], F32, name=f"plain{half}{r}")
-            nc.scalar.activation(plain[:], y_t[half][:].indirect(pos_t[r][:]), COPY)
+            for cols in pieces:
+                nc.scalar.activation(plain[:, cols], y_t[half][:].indirect(listed(r, cols)), COPY)
             return plain
 
         def weigh(r, plain, term, cols):
@@ -332,7 +348,8 @@ def tile_moe_tk_mlp_relu_kernel(
                 nc.scalar.copy(out=summed[:, b, :], in_=acc[b][:])
                 nc.tensor.transpose(back[b], summed[:, b, :], ident[:])
 
-        plain = {(half, r): fetch_plain(half, r) for half in range(2) for r in (2, 3)}
+        plain = {(half, r): fetch_plain(half, r, [whole]) for half, r in ((0, 2), (0, 3), (1, 2))}
+        plain[1, 3] = fetch_plain(1, 3, blocks)
 
         acc = [bank(n, [P, C]) for n in (5, 6, 7)]
         for r in range(TOP):

@@ -18,7 +18,7 @@ COPY = mybir.ActivationFunctionType.Copy
 K, T, E, C, H, N, TOP = 1024, 384, 12, 128, 512, 256, 4
 P = 128
 PASSES = K // 512
-WORD_WINDOW = 512
+WORD_WINDOW = 704
 BYTE_WINDOW = 1024
 ROWS_A_LOAD = (2, 4)
 VECTOR_TOKENS = 288
@@ -261,19 +261,18 @@ def tile_moe_tk_mlp_relu_kernel(
         second_pass_words(0, 2)
         second_pass_bytes(2, 8)
         second_pass_words(2, 4)
-        first_pass_words(4, 7)
+        first_pass_words(4, 8)
         second_pass_words(4, 6)
         first_pass_bytes(6, 10)
-        second_pass_words(6, 7)
-        first_pass_words(7, 10)
-        second_pass_words(7, 8)
+        second_pass_words(6, 8)
+        first_pass_words(8, 11)
         second_pass_bytes(8, 10)
         second_pass_words(8, 10)
         first_pass_bytes(10, E)
         second_pass_bytes(10, E)
-        for e in (10, 11):
-            first_pass_words(e, e + 1)
-            second_pass_words(e, e + 1)
+        second_pass_words(10, 11)
+        first_pass_words(11, E)
+        second_pass_words(11, E)
 
         pos_t = []
         for a in range(0, E, 2):
@@ -317,8 +316,8 @@ def tile_moe_tk_mlp_relu_kernel(
         second_product(1, 4, 8, 1, on_scalar)
         second_product(0, 8, 10, 0, on_vector)
         second_product(0, 10, E, 3, on_vector)
-        second_product(1, 11, E, 5, on_vector)
-        second_product(1, 8, 11, 4, on_scalar)
+        second_product(1, 8, 10, 4, on_scalar)
+        second_product(1, 10, E, 5, on_vector)
 
         whole = slice(0, T)
         blocks = [slice(C * b, C * (b + 1)) for b in range(T // C)]

@@ -58,13 +58,13 @@ def tile_moe_tk_mlp_relu_kernel(
             count = ROWS_A_LOAD[s]
             parts = []
             for d in range(0, 4, count):
-                part = keep.tile([P, count, T], F32, name=f"raw{s}{d}", align_bytes=64)
+                part = keep.tile([P, count, T], F32, name=f"raw{s}{d}", align_bytes=256)
                 nc.sync.dma_start(out=part[:], in_=rows[:, d : d + count, :])
                 parts.append((slice(d, d + count), part))
             x_parts.append(parts)
 
         def load_w1_pair(a):
-            w = keep.tile([P, 2, PASSES, 2 * H], U8, name=f"w1w{a}", align_bytes=64)
+            w = keep.tile([P, 2, PASSES, 2 * H], U8, name=f"w1w{a}", align_bytes=256)
             nc.sync.dma_start(
                 out=w[:].rearrange("p e s w -> p (e s) w").bitcast(I32),
                 in_=w1_words32[a : a + 2].rearrange("e s p w -> p (e s) w"),
@@ -298,7 +298,7 @@ def tile_moe_tk_mlp_relu_kernel(
                 out=w2_plane[r:P:32].bitcast(I32),
                 in_=w2_scales32[:, 0, r:16:4, :].rearrange("e q n -> q e n"),
             )
-        gate_t = keep.tile([P, TOP, T], F32, name="gate_t", align_bytes=64)
+        gate_t = keep.tile([P, TOP, T], F32, name="gate_t", align_bytes=256)
         nc.sync.dma_start(out=gate_t[:], in_=gate[:, 0:P, :].rearrange("r p t -> p r t"))
 
         quantise_hidden(0, 4, quads[0], "hb0")
@@ -350,15 +350,22 @@ def tile_moe_tk_mlp_relu_kernel(
         plain = {(half, r): fetch_plain(half, r, [whole]) for half, r in ((0, 2), (0, 3), (1, 2))}
         plain[1, 3] = fetch_plain(1, 3, blocks)
 
-        acc = [bank(n, [P, C]) for n in (5, 6, 7)]
+        first_acc = bank(6, [P, T])
         for r in range(TOP):
             term = keep.tile([P, T], F32, name=f"term0{r}")
             if r < 2:
                 fetch(0, r, term, whole)
             else:
                 weigh(r, plain[0, r], term, whole)
-            add_on_tensor(acc, term, r == 0, r == TOP - 1)
-        first_acc = acc
+            for b, cols in enumerate(blocks):
+                nc.tensor.matmul(
+                    first_acc[:, cols],
+                    lhsT=term[:, cols],
+                    rhs=ident[:],
+                    is_transpose=True,
+                    start=(r == 0 and b == 0),
+                    stop=(r == TOP - 1 and b == len(blocks) - 1),
+                )
 
         acc = [bank(n, [P, C]) for n in (0, 1, 2)]
         term = keep.tile([P, T], F32, name="plain02")
@@ -372,7 +379,10 @@ def tile_moe_tk_mlp_relu_kernel(
             weigh(3, plain[1, 3], term, cols)
         add_on_tensor(acc, term, False, True)
         back = bank(3, [P, T])
-        turn_back("summed0", first_acc, [back[:, cols] for cols in blocks])
+        summed = keep.tile([P, T], F32, name="summed0")
+        nc.scalar.copy(out=summed[:], in_=first_acc[:])
+        for cols in blocks:
+            nc.tensor.transpose(back[:, cols], summed[:, cols], ident[:])
         pieces = (slice(0, 2 * C), slice(2 * C, T))
         backs = [bank(4, [P, 2 * C]), bank(5, [P, C])]
         turn_back("summed1", acc, [backs[0][:, :C], backs[0][:, C:], backs[1][:]])

@@ -22,6 +22,7 @@ WORD_WINDOW = 704
 BYTE_WINDOW = 1024
 ROWS_A_LOAD = (2, 4)
 VECTOR_TOKENS = 288
+LAST_TOKENS = 32
 EARLY_BYTES = 6
 EARLY_WORDS = 4
 LATE_BYTES_AT = 2048
@@ -142,13 +143,25 @@ def tile_moe_tk_mlp_relu_kernel(
                 quantise_tokens(0, cols, rounded[:, cols, :])
 
         def second_pass_tokens():
-            for cols in (slice(0, 2 * C), slice(2 * C, T)):
-                rounded = shared.tile(
-                    [P, cols.stop - cols.start, 4], BF16, name=f"rounded{cols.start}", align_bytes=64, offset=8 * cols.start
+            raw = x_parts[1][0][1]
+            pieces = (slice(0, 2 * C), slice(2 * C, T))
+            wide, narrow = (
+                shared.tile(
+                    [P, cols.stop - cols.start, 4],
+                    BF16,
+                    name=f"rounded{cols.start}",
+                    align_bytes=64,
+                    offset=8 * cols.start,
                 )
-                nc.scalar.activation(
-                    by_fours(rounded[:], "p (c i) d"), by_fours(x_parts[1][0][1][:, :, cols], "p d (c i)"), COPY
-                )
+                for cols in pieces
+            )
+            for rounded, a, b in (
+                (narrow[:, : C - LAST_TOKENS], 2 * C, T - LAST_TOKENS),
+                (wide[:], 0, 2 * C),
+                (narrow[:, C - LAST_TOKENS :], T - LAST_TOKENS, T),
+            ):
+                nc.scalar.activation(by_fours(rounded, "p (c i) d"), by_fours(raw[:, :, a:b], "p d (c i)"), COPY)
+            for cols, rounded in zip(pieces, (wide, narrow)):
                 quantise_tokens(1, cols, rounded[:])
 
         y_t = [keep.tile([P, TOP * T], F32, name=f"y_t{half}") for half in range(2)]
@@ -341,8 +354,8 @@ def tile_moe_tk_mlp_relu_kernel(
             for b, cols in enumerate(blocks):
                 nc.tensor.matmul(acc[b][:], lhsT=term[:, cols], rhs=ident[:], is_transpose=True, start=first, stop=last)
 
-        def turn_back(tag, acc, back):
-            summed = keep.tile([P, len(blocks), C], F32, name=tag)
+        def turn_back(acc, back):
+            summed = keep.tile([P, len(blocks), C], F32, name="summed1")
             for b in range(len(blocks)):
                 nc.scalar.copy(out=summed[:, b, :], in_=acc[b][:])
                 nc.tensor.transpose(back[b], summed[:, b, :], ident[:])
@@ -379,13 +392,13 @@ def tile_moe_tk_mlp_relu_kernel(
             weigh(3, plain[1, 3], term, cols)
         add_on_tensor(acc, term, False, True)
         back = bank(3, [P, T])
-        summed = keep.tile([P, T], F32, name="summed0")
-        nc.scalar.copy(out=summed[:], in_=first_acc[:])
+        first_sum = keep.tile([P, T], F32, name="summed0")
+        nc.scalar.copy(out=first_sum[:], in_=first_acc[:])
         for cols in blocks:
-            nc.tensor.transpose(back[:, cols], summed[:, cols], ident[:])
+            nc.tensor.transpose(back[:, cols], first_sum[:, cols], ident[:])
         pieces = (slice(0, 2 * C), slice(2 * C, T))
         backs = [bank(4, [P, 2 * C]), bank(5, [P, C])]
-        turn_back("summed1", acc, [backs[0][:, :C], backs[0][:, C:], backs[1][:]])
+        turn_back(acc, [backs[0][:, :C], backs[0][:, C:], backs[1][:]])
         total = [keep.tile([P, T], F32, name="term13"), keep.tile([P, T], F32, name="total1")]
         nc.scalar.copy(out=total[0][:], in_=back[:])
         nc.sync.dma_start(out=out[0:P, :], in_=total[0][:])

@@ -21,7 +21,7 @@ PASSES = K // 512
 WORD_WINDOW = 704
 BYTE_WINDOW = 1024
 ROWS_A_LOAD = (2, 4)
-VECTOR_TOKENS = 288
+VECTOR_TOKENS = 336
 LAST_TOKENS = 32
 EARLY_BYTES = 6
 EARLY_WORDS = 4

from contextlib import ExitStack

import concourse.mybir as mybir
from concourse.masks import make_identity

F32 = mybir.dt.float32
BF16 = mybir.dt.bfloat16
I32 = mybir.dt.int32
U32 = mybir.dt.uint32
U16 = mybir.dt.uint16
U8 = mybir.dt.uint8
FP8X4 = mybir.dt.float8_e4m3fn_x4
FP4X4 = mybir.dt.float4_e2m1fn_x4
MULT = mybir.AluOpType.mult
RELU = mybir.ActivationFunctionType.Relu
COPY = mybir.ActivationFunctionType.Copy

K, T, E, C, H, N, TOP = 1024, 384, 12, 128, 512, 256, 4
P = 128
PASSES = K // 512
WORD_WINDOW = 704
BYTE_WINDOW = 1024
ROWS_A_LOAD = (2, 4)
VECTOR_TOKENS = 336
LAST_TOKENS = 32
EARLY_BYTES = 6
EARLY_WORDS = 4
LATE_BYTES_AT = 2048
LATE_WORDS_AT = 2816
FLOPS = 2 * TOP * T * (K * H + H * N)


def tile_moe_tk_mlp_relu_kernel(
    tc, xT, w1_words, w1_scales, w2_words, w2_scales, gate, offs, pos1, pos2, pos3, pos4, out
):
    nc = tc.nc
    with ExitStack() as ctx:
        keep = ctx.enter_context(tc.tile_pool(name="keep", bufs=1))
        shared = ctx.enter_context(tc.tile_pool(name="shared", bufs=1))
        psum = ctx.enter_context(tc.psum_pool(name="psum", bufs=1))

        def bank(n, shape):
            return psum.tile(shape, F32, name=f"bank{n}")

        on_scalar = nc.scalar.copy
        on_vector = nc.vector.tensor_copy

        w1_words32 = w1_words.bitcast(I32)
        w1_scales32 = w1_scales.bitcast(I32)
        w2_words32 = w2_words.bitcast(I32)
        w2_scales32 = w2_scales.bitcast(I32)
        x_parts = []
        w1_at = {}
        w1_plane_at = {}
        w2_at = {}

        def load_x(s):
            rows = xT[512 * s : 512 * (s + 1), :].rearrange("(p d) t -> p d t", d=4)
            count = ROWS_A_LOAD[s]
            parts = []
            for d in range(0, 4, count):
                part = keep.tile([P, count, T], F32, name=f"raw{s}{d}", align_bytes=256)
                nc.sync.dma_start(out=part[:], in_=rows[:, d : d + count, :])
                parts.append((slice(d, d + count), part))
            x_parts.append(parts)

        def load_w1_pair(a):
            w = keep.tile([P, 2, PASSES, 2 * H], U8, name=f"w1w{a}", align_bytes=256)
            nc.sync.dma_start(
                out=w[:].rearrange("p e s w -> p (e s) w").bitcast(I32),
                in_=w1_words32[a : a + 2].rearrange("e s p w -> p (e s) w"),
            )
            for e in range(2):
                w1_at[a + e] = w[:, e]
            return w

        def zeroed_plane(a, b):
            plane = keep.tile([P, b - a, PASSES, H], U8, name=f"w1s{a}", align_bytes=64)
            nc.vector.memset(plane[:].rearrange("p e s i -> p (e s i)").bitcast(I32), 0)
            return plane

        def load_w1_scales(a, b, plane):
            for r in range(4):
                nc.sync.dma_start(
                    out=plane[r:P:32].rearrange("p e s i -> p (e s) i").bitcast(I32),
                    in_=w1_scales32[a:b, :, r:16:4, :].rearrange("e s q i -> q (e s) i"),
                )
            for e in range(a, b):
                w1_plane_at[e] = plane[:, e - a]

        def load_w2(a, b):
            w = keep.tile([P, b - a, 2 * N], U8, name=f"w2w{a}", align_bytes=64)
            nc.sync.dma_start(out=w[:].bitcast(I32), in_=w2_words32[a:b, 0].rearrange("e p w -> p e w"))
            for e in range(a, b):
                w2_at[e] = w[:, e - a]

        ident = keep.tile([P, P], F32, name="ident")
        make_identity(nc, ident[:])

        load_x(0)
        offs_t = keep.tile([P, TOP * T // 16], U16, name="offs_t")
        nc.sync.dma_start(offs_t[:], offs)
        load_x(1)
        first_words = load_w1_pair(0)
        load_w1_pair(2)
        first_plane = zeroed_plane(0, 4)
        load_w1_scales(0, 4, first_plane)
        load_w1_scales(4, 8, zeroed_plane(4, 8))
        load_w1_pair(4)
        load_w1_pair(6)

        all_bytes = keep.tile([P, T + BYTE_WINDOW], U8, name="all_bytes", align_bytes=64)
        all_words = keep.tile([P, T + WORD_WINDOW], I32, name="all_words", align_bytes=64)
        nc.vector.memset(all_bytes[:, 2 * T :].bitcast(I32), 0)
        nc.vector.memset(all_words[:, 2 * T :], 0)
        byte_window = [all_bytes[:, T:], all_bytes[:, :BYTE_WINDOW]]
        word_window = [all_words[:, T:], all_words[:, :WORD_WINDOW]]

        def by_fours(view, order):
            return view.rearrange(order + " -> p c d i", i=4)

        def quantise_tokens(s, cols, rounded):
            nc.vector.quantize_mx(
                out=word_window[s][:, cols].bitcast(FP8X4),
                scales=byte_window[s][:, cols],
                in_=rounded.rearrange("p t d -> p (t d)"),
            )

        def first_pass_tokens():
            rounded = keep.tile([P, T, 4], BF16, name="rounded", align_bytes=64)
            shares = [[(0, VECTOR_TOKENS)], [(0, C), (C, VECTOR_TOKENS)]]
            for share, (rows, part) in zip(shares, x_parts[0]):
                for a, b in share:
                    nc.vector.tensor_copy(
                        out=by_fours(rounded[:, a:b, rows], "p (c i) d"), in_=by_fours(part[:, :, a:b], "p d (c i)")
                    )
                nc.scalar.activation(
                    by_fours(rounded[:, VECTOR_TOKENS:, rows], "p (c i) d"),
                    by_fours(part[:, :, VECTOR_TOKENS:], "p d (c i)"),
                    COPY,
                )
            for cols in (slice(0, C), slice(C, T)):
                quantise_tokens(0, cols, rounded[:, cols, :])

        def second_pass_tokens():
            raw = x_parts[1][0][1]
            pieces = (slice(0, 2 * C), slice(2 * C, T))
            wide, narrow = (
                shared.tile(
                    [P, cols.stop - cols.start, 4],
                    BF16,
                    name=f"rounded{cols.start}",
                    align_bytes=64,
                    offset=8 * cols.start,
                )
                for cols in pieces
            )
            for rounded, a, b in (
                (narrow[:, : C - LAST_TOKENS], 2 * C, T - LAST_TOKENS),
                (wide[:], 0, 2 * C),
                (narrow[:, C - LAST_TOKENS :], T - LAST_TOKENS, T),
            ):
                nc.scalar.activation(by_fours(rounded, "p (c i) d"), by_fours(raw[:, :, a:b], "p d (c i)"), COPY)
            for cols, rounded in zip(pieces, (wide, narrow)):
                quantise_tokens(1, cols, rounded[:])

        y_t = [keep.tile([P, TOP * T], F32, name=f"y_t{half}") for half in range(2)]
        bytes_at = {}
        words_at = {}
        act_at = {}
        hidden_at = {}

        def gather_bytes(s, a, b, tile, first):
            slots = tile[:, C * (a - first) : C * (b - first)]
            nc.vector.tensor_copy(slots, byte_window[s].indirect(offs_t[:, C // 16 * a : C // 16 * b]))
            for e in range(a, b):
                bytes_at[e, s] = slots[:, C * (e - a) : C * (e - a + 1)]

        def gather_words(s, a, b, tile, first):
            slots = tile[:, C * (a - first) : C * (b - first)]
            nc.vector.tensor_copy(slots, word_window[s].bitcast(U32).indirect(offs_t[:, C // 16 * a : C // 16 * b]))
            for e in range(a, b):
                words_at[e, s] = slots[:, C * (e - a) : C * (e - a + 1)]

        def first_product(e):
            acc = bank(e % 4, [P, H])
            for s in range(PASSES):
                nc.tensor.matmul_mx(
                    out=acc[:],
                    lhsT=words_at[e, s].bitcast(FP8X4),
                    lhsT_scale=bytes_at[e, s],
                    rhs=w1_at[e][:, s, :].bitcast(FP4X4),
                    rhs_scale=w1_plane_at[e][:, s, :],
                    start=(s == 0),
                    stop=(s == PASSES - 1),
                )
            act = keep.tile([P, H], BF16, name=f"act{e}", align_bytes=64)
            nc.scalar.activation(
                act[:].rearrange("p (u m j) -> p u m j", u=2, j=2),
                acc[:].rearrange("p (m u j) -> p u m j", u=2, j=2),
                RELU,
            )
            act_at[e] = act

        def turn(a, b, n, hidden, copy):
            turned = bank(n, [P, b - a, 2, C])
            for e in range(a, b):
                for u in range(2):
                    nc.tensor.transpose(
                        turned[:, e - a, u, :], act_at[e][:].bitcast(F32)[:, C * u : C * (u + 1)], ident[:]
                    )
            copy(
                out=hidden.bitcast(F32).rearrange("p (e c u) -> p e c u", e=b - a, u=2),
                in_=turned[:].rearrange("p e u c -> p e c u"),
            )

        def hidden_tile(a, b):
            return keep.tile([P, (b - a) * H], BF16, name=f"ht{a}", align_bytes=64)

        def quantise_hidden(a, b, hidden, plane_tag):
            words = keep.tile([P, (b - a) * C], U32, name=f"hw{a}", align_bytes=64)
            plane = keep.tile([P, (b - a) * C], U8, name=plane_tag, align_bytes=64)
            nc.vector.quantize_mx(out=words[:].bitcast(FP8X4), scales=plane[:], in_=hidden[:])
            for e in range(a, b):
                cols = slice(C * (e - a), C * (e - a + 1))
                hidden_at[e] = (words[:, cols], plane[:, cols])

        def second_product(half, a, b, n, copy):
            sums = bank(n, [P, (b - a) * C])
            for e in range(a, b):
                words, plane = hidden_at[e]
                nc.tensor.matmul_mx(
                    out=sums[:, C * (e - a) : C * (e - a + 1)],
                    lhsT=w2_at[e][:, 2 * P * half : 2 * P * (half + 1)].bitcast(FP4X4),
                    lhsT_scale=w2_plane[:, e, P * half : P * (half + 1)],
                    rhs=words.bitcast(FP8X4),
                    rhs_scale=plane,
                    start=True,
                    stop=True,
                )
            copy(out=y_t[half][:, C * a : C * b], in_=sums[:])

        first_pass_tokens()
        early_bytes = keep.tile([P, EARLY_BYTES * C], U8, name="early_bytes", align_bytes=64)
        early_words = keep.tile([P, 2 * C], U32, name="early_words", align_bytes=64)
        gather_words(0, 0, 2, early_words, 0)
        gather_bytes(0, 0, EARLY_BYTES, early_bytes, 0)
        second_pass_tokens()
        between = shared.tile([P, 2 * C], U32, name="between", align_bytes=64, offset=0)
        gather_words(0, 2, EARLY_WORDS, between, 2)
        late_bytes = shared.tile(
            [P, (E - EARLY_BYTES) * C], U8, name="late_bytes", align_bytes=64, offset=LATE_BYTES_AT
        )
        late_words = shared.tile(
            [P, (E - EARLY_WORDS) * C], U32, name="late_words", align_bytes=64, offset=LATE_WORDS_AT
        )
        second_bytes = keep.tile([P, E * C], U8, name="second_bytes", align_bytes=64)
        second_words = keep.tile([P, E * C], U32, name="second_words", align_bytes=64)
        quads = [hidden_tile(0, 4), hidden_tile(4, 8)]

        def first_pass_bytes(a, b):
            gather_bytes(0, a, b, late_bytes, EARLY_BYTES)

        def first_pass_words(a, b):
            gather_words(0, a, b, late_words, EARLY_WORDS)

        def second_pass_bytes(a, b):
            gather_bytes(1, a, b, second_bytes, 0)

        def second_pass_words(a, b):
            gather_words(1, a, b, second_words, 0)

        second_pass_bytes(0, 2)
        second_pass_words(0, 2)
        second_pass_bytes(2, 8)
        second_pass_words(2, 4)
        first_pass_words(4, 8)
        second_pass_words(4, 6)
        first_pass_bytes(6, 10)
        second_pass_words(6, 8)
        first_pass_words(8, 11)
        second_pass_bytes(8, 10)
        second_pass_words(8, 10)
        first_pass_bytes(10, E)
        second_pass_bytes(10, E)
        second_pass_words(10, 11)
        first_pass_words(11, E)
        second_pass_words(11, E)

        pos_t = []
        for a in range(0, E, 2):
            first_product(a)
            first_product(a + 1)
            if a == 0:
                load_w1_scales(8, E, first_words[:].rearrange("p e s (g i) -> p (e s) g i", g=PASSES))
                load_w1_pair(8)
                load_w1_pair(10)
                load_w2(0, 8)
                load_w2(8, E)
                for r, pos in enumerate((pos1, pos2, pos3, pos4)):
                    listed = keep.tile([P, T // 16], U16, name=f"pos_t{r}")
                    nc.sync.dma_start(listed[:], pos)
                    pos_t.append(listed)
            if 2 <= a <= 8:
                place = (a - 2) % 4
                turn(a - 2, a, 4 + a // 2 % 2, quads[(a - 2) // 4][:, H * place : H * (place + 2)], on_scalar)

        w2_plane = first_plane[:].rearrange("p e s i -> p (e s i)")[:, : E * N].rearrange("p (e n) -> p e n", n=N)
        for r in range(4):
            nc.sync.dma_start(
                out=w2_plane[r:P:32].bitcast(I32),
                in_=w2_scales32[:, 0, r:16:4, :].rearrange("e q n -> q e n"),
            )
        gate_t = keep.tile([P, TOP, T], F32, name="gate_t", align_bytes=256)
        nc.sync.dma_start(out=gate_t[:], in_=gate[:, 0:P, :].rearrange("r p t -> p r t"))

        quantise_hidden(0, 4, quads[0], "hb0")
        pair, tenth, eleventh = hidden_tile(8, 10), hidden_tile(10, 11), hidden_tile(11, E)
        turn(8, 10, 0, pair[:], on_vector)
        quantise_hidden(4, 8, quads[1], "hb4")
        turn(10, 11, 4, tenth[:], on_scalar)
        turn(11, E, 5, eleventh[:], on_scalar)
        quantise_hidden(10, 11, tenth, "hb10")
        quantise_hidden(8, 10, pair, "act11")
        quantise_hidden(11, E, eleventh, "hb11")
        second_product(1, 0, 4, 6, on_scalar)
        second_product(0, 0, 4, 7, on_vector)
        second_product(0, 4, 8, 2, on_scalar)
        second_product(1, 4, 8, 1, on_scalar)
        second_product(0, 8, 10, 0, on_vector)
        second_product(0, 10, E, 3, on_vector)
        second_product(1, 8, 10, 4, on_scalar)
        second_product(1, 10, E, 5, on_vector)

        whole = slice(0, T)
        blocks = [slice(C * b, C * (b + 1)) for b in range(T // C)]

        def listed(r, cols):
            return pos_t[r][:, cols.start // 16 : cols.stop // 16]

        def fetch(half, r, term, cols):
            nc.vector.tensor_tensor(term[:, cols], y_t[half][:].indirect(listed(r, cols)), gate_t[:, r, cols], MULT)

        def fetch_plain(half, r, pieces):
            plain = keep.tile([P, T], F32, name=f"plain{half}{r}")
            for cols in pieces:
                nc.scalar.activation(plain[:, cols], y_t[half][:].indirect(listed(r, cols)), COPY)
            return plain

        def weigh(r, plain, term, cols):
            nc.vector.tensor_tensor(term[:, cols], plain[:, cols], gate_t[:, r, cols], MULT)

        def add_on_tensor(acc, term, first, last):
            for b, cols in enumerate(blocks):
                nc.tensor.matmul(acc[b][:], lhsT=term[:, cols], rhs=ident[:], is_transpose=True, start=first, stop=last)

        def turn_back(acc, back):
            summed = keep.tile([P, len(blocks), C], F32, name="summed1")
            for b in range(len(blocks)):
                nc.scalar.copy(out=summed[:, b, :], in_=acc[b][:])
                nc.tensor.transpose(back[b], summed[:, b, :], ident[:])

        plain = {(half, r): fetch_plain(half, r, [whole]) for half, r in ((0, 2), (0, 3), (1, 2))}
        plain[1, 3] = fetch_plain(1, 3, blocks)

        first_acc = bank(6, [P, T])
        for r in range(TOP):
            term = keep.tile([P, T], F32, name=f"term0{r}")
            if r < 2:
                fetch(0, r, term, whole)
            else:
                weigh(r, plain[0, r], term, whole)
            for b, cols in enumerate(blocks):
                nc.tensor.matmul(
                    first_acc[:, cols],
                    lhsT=term[:, cols],
                    rhs=ident[:],
                    is_transpose=True,
                    start=(r == 0 and b == 0),
                    stop=(r == TOP - 1 and b == len(blocks) - 1),
                )

        acc = [bank(n, [P, C]) for n in (0, 1, 2)]
        term = keep.tile([P, T], F32, name="plain02")
        fetch(1, 0, term, whole)
        add_on_tensor(acc, term, True, False)
        term = keep.tile([P, T], F32, name="term12")
        weigh(2, plain[1, 2], term, whole)
        add_on_tensor(acc, term, False, False)
        term = keep.tile([P, T], F32, name="term13")
        for cols in blocks:
            weigh(3, plain[1, 3], term, cols)
        add_on_tensor(acc, term, False, True)
        back = bank(3, [P, T])
        first_sum = keep.tile([P, T], F32, name="summed0")
        nc.scalar.copy(out=first_sum[:], in_=first_acc[:])
        for cols in blocks:
            nc.tensor.transpose(back[:, cols], first_sum[:, cols], ident[:])
        pieces = (slice(0, 2 * C), slice(2 * C, T))
        backs = [bank(4, [P, 2 * C]), bank(5, [P, C])]
        turn_back(acc, [backs[0][:, :C], backs[0][:, C:], backs[1][:]])
        total = [keep.tile([P, T], F32, name="term13"), keep.tile([P, T], F32, name="total1")]
        nc.scalar.copy(out=total[0][:], in_=back[:])
        nc.sync.dma_start(out=out[0:P, :], in_=total[0][:])
        last = keep.tile([P, T], F32, name="plain12")
        for cols in pieces:
            fetch(1, 1, last, cols)
        for b, cols in enumerate(pieces):
            nc.vector.tensor_add(total[1][:, cols], last[:, cols], backs[b][:])
            nc.sync.dma_start(out=out[P:, cols], in_=total[1][:, cols])
